import numpy as np
import ml_dtypes


def mxq(x, axis, fmt="e4m3"):
    dtype, down = {"e4m3": (ml_dtypes.float8_e4m3fn, 7), "e5m2": (ml_dtypes.float8_e5m2, 14)}[fmt]
    v = np.moveaxis(np.asarray(x, np.float32).astype(ml_dtypes.bfloat16).astype(np.float64), axis, -1)
    blocks = v.reshape(v.shape[:-1] + (-1, 32))
    amax = np.abs(blocks).max(-1, keepdims=True)
    byte = np.maximum(np.where(amax > 0, np.frexp(amax)[1] - 1 + 127, 0) - down, 1)
    scale = np.exp2(byte - 127.0)
    codes = (blocks / scale).astype(np.float32).astype(dtype).astype(np.float64)
    return np.moveaxis((codes * scale).reshape(v.shape), -1, axis)


WIDE = False


def mx_kscale(k):
    if not WIDE:
        return np.ones(k)
    levels = np.array([10, -10, 5, -5, 0])
    if k % 512:
        return np.exp2(np.random.permutation(np.resize(levels, k // 32))).repeat(32)
    a = np.empty((k // 512, 16))
    for p in range(k // 512):
        a[p, :8] = np.random.permutation(np.resize(levels, 8))
        for g in range(8):
            far = levels[np.abs(levels - a[p, g]) >= 10]
            a[p, g + 8] = far[np.random.randint(len(far))]
    return np.exp2(a.ravel()).repeat(32)


def f64(x):
    return np.asarray(x).astype(np.float64)


def striped(idx):
    return np.tile(idx.reshape(-1, 16).T, (8, 1)).astype(np.uint16)


def unstriped(offs):
    return offs[:16].T.reshape(-1).astype(np.int64)


def striped8(idx):
    return np.concatenate([x.reshape(-1, 16).T for x in idx]).astype(np.uint16)


def runs(offs, k):
    lists = np.stack([offs[16 * r : 16 * r + 16].T.reshape(-1) for r in range(8)]).astype(np.int64)
    return lists[np.arange(k) % 512 // 64]


def pack_weight(w):
    k, n = w.shape
    w = f64(np.asarray(w, np.float32).astype(ml_dtypes.bfloat16)).reshape(k // 32, 32, n)
    amax = np.abs(w).max(1)
    byte = np.clip(np.where(amax > 0, np.frexp(amax)[1] - 1 + 127 - 7, 1), 1, 254)
    scaled = (w * np.exp2(127.0 - byte)[:, None, :]).reshape(k, n).astype(np.float32)
    words = np.ascontiguousarray(scaled.reshape(k // 512, 128, 4, n).transpose(0, 1, 3, 2)).astype(ml_dtypes.float8_e4m3fn).view(np.uint8)
    return words, np.ascontiguousarray(byte.astype(np.uint8).reshape(k // 512, 16, n))


def unpack_weight(words, scales):
    g, p, n, _ = words.shape
    vals = np.ascontiguousarray(words).view(ml_dtypes.float8_e4m3fn).astype(np.float64) * np.repeat(np.exp2(scales.astype(np.float64) - 127.0), 8, axis=1)[..., None]
    return vals.transpose(0, 1, 3, 2).reshape(g * 512, n)


K, T, S, N, H, U = 512, 2048, 512, 512, 512, 1024


def setup_inputs():
    n = np.random.standard_normal
    s = mx_kscale(K)[:, None]
    u = mx_kscale(H)
    packed_xT = pack_weight(n((K, T)) * s)
    perm = np.stack([np.random.permutation(U) for _ in range(8)])
    return {
        "x_words": packed_xT[0],
        "x_scales": packed_xT[1],
        "w1": (n((K, H)) / np.sqrt(K) / s * u).astype(np.float32),
        "w2": (n((K, H)) / np.sqrt(K) / s * u).astype(np.float32),
        "w3": (n((H, N)) / np.sqrt(H) / u[:, None]).astype(np.float32),
        "offs": striped(np.random.permutation(T)[:S]),
        "img": striped(np.random.permutation(T)[:S]),
        "la": striped8(perm[:, :S]),
        "lb": striped8(perm[:, S:]),
    }


def reference(x_words, x_scales, w1, w2, w3, offs, img, la, lb):
    x_img = unpack_weight(x_words, x_scales)[:, unstriped(img)]
    e = mxq(f64(w2), 0, "e4m3").T @ x_img
    xq = unpack_weight(x_words, x_scales)[:, unstriped(offs)]
    y = mxq(f64(w1), 0, "e4m3").T @ xq
    p = np.zeros((H, U))
    p[np.arange(H)[:, None], runs(la, H)] = y
    z = p.copy()
    z[np.arange(H)[:, None], runs(lb, H)] = e
    return mxq(f64(w3), 0, "e4m3").T @ mxq(z, 0, "e4m3")

@@ -1,0 +1,172 @@
+from contextlib import ExitStack
+
+import concourse.mybir as mybir
+
+K, T, S, H, N, U = 512, 2048, 512, 512, 512, 1024
+FLOPS = 2 * K * H * S * 2 + 2 * H * N * U
+
+F32 = mybir.dt.float32
+BF16 = mybir.dt.bfloat16
+I32 = mybir.dt.int32
+U32 = mybir.dt.uint32
+U16 = mybir.dt.uint16
+U8 = mybir.dt.uint8
+FP8X4 = mybir.dt.float8_e4m3fn_x4
+
+P = 128
+PACK = 4
+PLANES = (1, 2, 3, 0)
+CHUNKS = (128, 128, 256, 256, 256)
+SHARED_FROM = 3
+
+
+def tile_picked_interl_none_p_kernel(
+    tc, x_words, x_scales, w1, w2, w3, offs, img, la, lb, out
+):
+    nc = tc.nc
+    with ExitStack() as ctx:
+        held = ctx.enter_context(tc.tile_pool(name="held", bufs=1))
+        psum = ctx.enter_context(tc.psum_pool(name="psum", bufs=8))
+
+        def load_list(source, name):
+            tile = held.tile([P, S // 16], U16, name=name)
+            nc.sync.dma_start(tile[:], source)
+            return tile
+
+        def load_weight(source, name):
+            tile = held.tile([P, PACK, H], F32, name=name)
+            nc.sync.dma_start(tile[:], source.rearrange("(p j) c -> p j c", j=PACK))
+            return tile
+
+        def quantise(values, name, tag=None):
+            width = values.shape[1] // PACK
+            codes = held.tile([P, width], U32, name=name + "_codes", tag=tag or name + "_codes", align_bytes=64)
+            scales = held.tile([P, width], U8, name=name + "_scales", align_bytes=64)
+            nc.vector.quantize_mx(out=codes[:].bitcast(FP8X4), scales=scales[:], in_=values)
+            return codes, scales
+
+        def multiply(bank, stationary, columns, moving):
+            nc.tensor.matmul_mx(
+                out=bank,
+                lhsT=stationary[0][:, columns].bitcast(FP8X4),
+                lhsT_scale=stationary[1][:, columns],
+                rhs=moving[0][:].bitcast(FP8X4),
+                rhs_scale=moving[1][:],
+                start=True,
+                stop=True,
+            )
+
+        def project(weights, columns, tokens, name, tag):
+            bank = psum.tile([P, S], F32, name="bank")
+            multiply(bank[:], weights, columns, tokens)
+            values = held.tile([P, S], F32, name=name, tag=tag, align_bytes=64)
+            nc.scalar.copy(values[:], bank[:])
+            return values
+
+        table_scales = held.tile([P, T], U8, name="table_scales")
+        nc.vector.memset(table_scales[:].bitcast(I32), 0)
+        text_list = load_list(offs, "text_list")
+        table_words = held.tile([P, T], U32, name="table_words")
+        nc.sync.dma_start(
+            table_words[:].bitcast(I32), x_words[0].rearrange("p c r -> p (c r)").bitcast(I32)
+        )
+        image_list = load_list(img, "image_list")
+        for q in range(4):
+            nc.sync.dma_start(
+                table_scales[32 * q : 32 * q + 4, :].bitcast(I32),
+                x_scales[0, 4 * q : 4 * q + 4, :].bitcast(I32),
+            )
+        w1_raw = load_weight(w1, "w1_raw")
+        text_places = load_list(la, "text_places")
+        w2_raw = load_weight(w2, "w2_raw")
+        image_places = load_list(lb, "image_places")
+        w3_raw = load_weight(w3, "w3_raw")
+
+        def gather(table, offsets, dtype, name, tag=None):
+            picked = held.tile([P, S], dtype, name=name, tag=tag or name, align_bytes=64)
+            nc.vector.tensor_copy(picked[:], table[:].indirect(offsets[:]))
+            return picked
+
+        text_words = gather(table_words, text_list, U32, "text_words")
+        image_words = gather(table_words, image_list, U32, "image_words")
+        text = (text_words, gather(table_scales, text_list, U8, "text_scales"))
+
+        def quantise_plane(raw, t, name):
+            rounded = held.tile([P, P * PACK], BF16, name=name + "_bf", align_bytes=64)
+            nc.scalar.copy(
+                rounded[:].rearrange("p (m j) -> p m j", j=PACK),
+                raw[:].rearrange("p j (m t) -> p t m j", t=PACK)[:, t],
+            )
+            return quantise(rounded[:], name)
+
+        w1_mx, y = {}, {}
+        for t in PLANES:
+            w1_mx[t] = quantise_plane(w1_raw, t, "w1_%d" % t)
+            if t != PLANES[-1]:
+                y[t] = project(w1_mx[t], slice(0, P), text, "y%d" % t, "y%d" % t)
+        image = (
+            image_words,
+            gather(table_scales, image_list, U8, "image_scales", "w1_%d_bf" % PLANES[0]),
+        )
+        z = {}
+
+        def place_text(t, tag):
+            z[t] = held.tile([P, U], F32, name="z%d" % t, tag=tag, align_bytes=64)
+            nc.vector.tensor_copy(z[t][:].indirect(text_places[:]), y[t][:])
+
+        place_text(PLANES[0], "z_first")
+        place_text(PLANES[1], "z_second")
+
+        w2_mx = {t: quantise_plane(w2_raw, t, "w2_%d" % t) for t in PLANES}
+        place_text(PLANES[2], "w2_%d_bf" % PLANES[0])
+        t = PLANES[-1]
+        y[t] = project(w1_mx[t], slice(0, P), text, "y%d" % t, "y%d" % t)
+        e = {}
+        t = PLANES[0]
+        e[t] = project(w2_mx[t], slice(0, P), image, "e%d" % t, "e%d" % t)
+
+        starts = [sum(CHUNKS[:i]) for i in range(len(CHUNKS))]
+        chunks = [slice(c, c + width) for c, width in zip(starts, CHUNKS)]
+        z_bf = [
+            held.tile([P, width, PACK], BF16, name="z_bf%d" % i, align_bytes=64)
+            for i, width in enumerate(CHUNKS)
+        ]
+
+        def plane(t):
+            return slice(P * t, P * (t + 1))
+
+
+        w3_bf = held.tile([P, PACK * N], BF16, name="w3_bf", tag="w3_bf", align_bytes=64)
+        for m in range(N // P):
+            nc.scalar.copy(
+                w3_bf[:].rearrange("p (c j) -> p c j", j=PACK)[:, plane(m), :],
+                w3_raw[:].rearrange("p j c -> p c j")[:, plane(m), :],
+            )
+
+        for t in PLANES[1:3]:
+            e[t] = project(w2_mx[t], slice(0, P), image, "e%d" % t, "e%d" % t)
+        for t in PLANES[:-1]:
+            nc.vector.tensor_copy(z[t][:].indirect(image_places[:]), e[t][:])
+            for i, columns in enumerate(chunks):
+                if t == PLANES[2] and i == 3:
+                    e_last = project(w2_mx[PLANES[3]], plane(0), image, "e_last", "z_second")
+                nc.scalar.copy(z_bf[i][:, :, t], z[t][:, columns])
+        t = PLANES[-1]
+        place_text(t, "e%d" % PLANES[1])
+        w3_mx = quantise(w3_bf[:], "w3", "e%d" % PLANES[2])
+        nc.vector.tensor_copy(z[t][:].indirect(image_places[:]), e_last[:])
+
+        out_rows = out.rearrange("(m p) w -> p m w", p=P)
+        for i, columns in enumerate(chunks):
+            nc.vector.tensor_copy(z_bf[i][:, :, t], z[t][:, columns])
+            z_mx = quantise(z_bf[i][:].rearrange("p c j -> p (c j)"), "z%d" % i)
+            for half in range(2):
+                bank = psum.tile([P, 2, CHUNKS[i]], F32, name="bank")
+                for m in range(2):
+                    multiply(bank[:, m, :], w3_mx, plane(2 * half + m), z_mx)
+                result = held.tile([P, 2, CHUNKS[i]], F32, name="result%d_%d" % (i, half))
+                if half == 1 and i >= SHARED_FROM:
+                    nc.vector.tensor_copy(result[:], bank[:])
+                else:
+                    nc.scalar.copy(result[:], bank[:])
+                nc.sync.dma_start(out_rows[:, 2 * half : 2 * half + 2, columns], result[:])

@@ -16,8 +16,7 @@ FP8X4 = mybir.dt.float8_e4m3fn_x4
 P = 128
 PACK = 4
 PLANES = (1, 2, 3, 0)
-CHUNKS = (128, 128, 256, 256, 256)
-SHARED_FROM = 3
+CHUNKS = (128, 128, 256, 512)
 
 
 def tile_picked_interl_none_p_kernel(
@@ -65,11 +64,11 @@ def tile_picked_interl_none_p_kernel(
 
         table_scales = held.tile([P, T], U8, name="table_scales")
         nc.vector.memset(table_scales[:].bitcast(I32), 0)
-        text_list = load_list(offs, "text_list")
         table_words = held.tile([P, T], U32, name="table_words")
         nc.sync.dma_start(
             table_words[:].bitcast(I32), x_words[0].rearrange("p c r -> p (c r)").bitcast(I32)
         )
+        text_list = load_list(offs, "text_list")
         image_list = load_list(img, "image_list")
         for q in range(4):
             nc.sync.dma_start(
@@ -152,21 +151,36 @@ def tile_picked_interl_none_p_kernel(
                     e_last = project(w2_mx[PLANES[3]], plane(0), image, "e_last", "z_second")
                 nc.scalar.copy(z_bf[i][:, :, t], z[t][:, columns])
         t = PLANES[-1]
-        place_text(t, "e%d" % PLANES[1])
-        w3_mx = quantise(w3_bf[:], "w3", "e%d" % PLANES[2])
+        place_text(t, "e%d" % PLANES[2])
+        w3_mx = quantise(w3_bf[:], "w3", "y%d" % t)
         nc.vector.tensor_copy(z[t][:].indirect(image_places[:]), e_last[:])
 
-        out_rows = out.rearrange("(m p) w -> p m w", p=P)
+        z_mx = []
         for i, columns in enumerate(chunks):
-            nc.vector.tensor_copy(z_bf[i][:, :, t], z[t][:, columns])
-            z_mx = quantise(z_bf[i][:].rearrange("p c j -> p (c j)"), "z%d" % i)
-            for half in range(2):
-                bank = psum.tile([P, 2, CHUNKS[i]], F32, name="bank")
-                for m in range(2):
-                    multiply(bank[:, m, :], w3_mx, plane(2 * half + m), z_mx)
-                result = held.tile([P, 2, CHUNKS[i]], F32, name="result%d_%d" % (i, half))
-                if half == 1 and i >= SHARED_FROM:
+            if i == len(chunks) - 1:
+                nc.scalar.copy(z_bf[i][:, :, t], z[t][:, columns])
+            else:
+                nc.vector.tensor_copy(z_bf[i][:, :, t], z[t][:, columns])
+            z_mx.append(quantise(z_bf[i][:].rearrange("p c j -> p (c j)"), "z%d" % i))
+
+        out_rows = out.rearrange("(m p) w -> p m w", p=P)
+        for half in range(2):
+            bank = psum.tile([P, 2, CHUNKS[0]], F32, name="bank")
+            for m in range(2):
+                multiply(bank[:, m, :], w3_mx, plane(2 * half + m), z_mx[0])
+            result = held.tile([P, 2, CHUNKS[0]], F32, name="result_a%d" % half)
+            nc.scalar.copy(result[:], bank[:])
+            nc.sync.dma_start(out_rows[:, 2 * half : 2 * half + 2, chunks[0]], result[:])
+        for group in ((1, 2), (3,)):
+            first, last = chunks[group[0]].start, chunks[group[-1]].stop
+            for m in range(N // P):
+                bank = psum.tile([P, last - first], F32, name="bank")
+                for i in group:
+                    within = slice(chunks[i].start - first, chunks[i].stop - first)
+                    multiply(bank[:, within], w3_mx, plane(m), z_mx[i])
+                result = held.tile([P, last - first], F32, name="result%d_%d" % (first, m))
+                if m % 2:
                     nc.vector.tensor_copy(result[:], bank[:])
                 else:
                     nc.scalar.copy(result[:], bank[:])
-                nc.sync.dma_start(out_rows[:, 2 * half : 2 * half + 2, columns], result[:])
+                nc.sync.dma_start(out[plane(m), first:last], result[:])

@@ -62,33 +62,36 @@ def tile_picked_interl_none_p_kernel(
             nc.scalar.copy(values[:], bank[:])
             return values
 
-        table_scales = held.tile([P, T], U8, name="table_scales")
-        nc.vector.memset(table_scales[:].bitcast(I32), 0)
+        scale_rows = held.tile([P, T], U8, name="scale_rows")
+        quadrants = [slice(32 * q, 32 * q + 4) for q in range(4)]
+        for q, rows in enumerate(quadrants):
+            nc.sync.dma_start(
+                scale_rows[rows, :].bitcast(I32), x_scales[0, 4 * q : 4 * q + 4, :].bitcast(I32)
+            )
+        text_list = load_list(offs, "text_list")
+        image_list = load_list(img, "image_list")
+        w1_raw = load_weight(w1, "w1_raw")
         table_words = held.tile([P, T], U32, name="table_words")
         nc.sync.dma_start(
             table_words[:].bitcast(I32), x_words[0].rearrange("p c r -> p (c r)").bitcast(I32)
         )
-        text_list = load_list(offs, "text_list")
-        image_list = load_list(img, "image_list")
-        for q in range(4):
-            nc.sync.dma_start(
-                table_scales[32 * q : 32 * q + 4, :].bitcast(I32),
-                x_scales[0, 4 * q : 4 * q + 4, :].bitcast(I32),
-            )
-        w1_raw = load_weight(w1, "w1_raw")
         text_places = load_list(la, "text_places")
         w2_raw = load_weight(w2, "w2_raw")
         image_places = load_list(lb, "image_places")
         w3_raw = load_weight(w3, "w3_raw")
 
-        def gather(table, offsets, dtype, name, tag=None):
-            picked = held.tile([P, S], dtype, name=name, tag=tag or name, align_bytes=64)
+        table_scales = held.tile([P, T], U8, name="table_scales")
+        nc.vector.memset(table_scales[:].bitcast(I32), 0)
+        for rows in quadrants:
+            nc.vector.tensor_copy(table_scales[rows, :].bitcast(I32), scale_rows[rows, :].bitcast(I32))
+
+        def gather(table, offsets, dtype, name):
+            picked = held.tile([P, S], dtype, name=name, align_bytes=64)
             nc.vector.tensor_copy(picked[:], table[:].indirect(offsets[:]))
             return picked
 
-        text_words = gather(table_words, text_list, U32, "text_words")
-        image_words = gather(table_words, image_list, U32, "image_words")
-        text = (text_words, gather(table_scales, text_list, U8, "text_scales"))
+        text_scales = gather(table_scales, text_list, U8, "text_scales")
+        image_scales = gather(table_scales, image_list, U8, "image_scales")
 
         def quantise_plane(raw, t, name):
             rounded = held.tile([P, P * PACK], BF16, name=name + "_bf", align_bytes=64)
@@ -98,15 +101,10 @@ def tile_picked_interl_none_p_kernel(
             )
             return quantise(rounded[:], name)
 
-        w1_mx, y = {}, {}
-        for t in PLANES:
-            w1_mx[t] = quantise_plane(w1_raw, t, "w1_%d" % t)
-            if t != PLANES[-1]:
-                y[t] = project(w1_mx[t], slice(0, P), text, "y%d" % t, "y%d" % t)
-        image = (
-            image_words,
-            gather(table_scales, image_list, U8, "image_scales", "w1_%d_bf" % PLANES[0]),
-        )
+        w1_mx = {t: quantise_plane(w1_raw, t, "w1_%d" % t) for t in PLANES}
+        text = (gather(table_words, text_list, U32, "text_words"), text_scales)
+        image = (gather(table_words, image_list, U32, "image_words"), image_scales)
+        y = {t: project(w1_mx[t], slice(0, P), text, "y%d" % t, "y%d" % t) for t in PLANES[:-1]}
         z = {}
 
         def place_text(t, tag):

@@ -15,8 +15,16 @@ FP8X4 = mybir.dt.float8_e4m3fn_x4
 
 P = 128
 PACK = 4
-PLANES = (1, 2, 3, 0)
+PSUM_BANKS = 8
+
+FIRST, SECOND, THIRD, LAST = PLANES = (1, 2, 3, 0)
+
 CHUNKS = (128, 128, 256, 512)
+STORES = ((0,), (1, 2), (3,))
+
+
+def block(index):
+    return slice(P * index, P * (index + 1))
 
 
 def tile_picked_interl_none_p_kernel(
@@ -25,7 +33,7 @@ def tile_picked_interl_none_p_kernel(
     nc = tc.nc
     with ExitStack() as ctx:
         held = ctx.enter_context(tc.tile_pool(name="held", bufs=1))
-        psum = ctx.enter_context(tc.psum_pool(name="psum", bufs=8))
+        psum = ctx.enter_context(tc.psum_pool(name="psum", bufs=PSUM_BANKS))
 
         def load_list(source, name):
             tile = held.tile([P, S // 16], U16, name=name)
@@ -33,20 +41,25 @@ def tile_picked_interl_none_p_kernel(
             return tile
 
         def load_weight(source, name):
-            tile = held.tile([P, PACK, H], F32, name=name)
+            tile = held.tile([P, PACK, H], F32, name=name, align_bytes=64)
             nc.sync.dma_start(tile[:], source.rearrange("(p j) c -> p j c", j=PACK))
             return tile
 
-        def quantise(values, name, tag=None):
-            width = values.shape[1] // PACK
-            codes = held.tile([P, width], U32, name=name + "_codes", tag=tag or name + "_codes", align_bytes=64)
-            scales = held.tile([P, width], U8, name=name + "_scales", align_bytes=64)
-            nc.vector.quantize_mx(out=codes[:].bitcast(FP8X4), scales=scales[:], in_=values)
-            return codes, scales
+        def gather(table, offsets, dtype, name):
+            picked = held.tile([P, S], dtype, name=name, align_bytes=64)
+            nc.vector.tensor_copy(picked[:], table[:].indirect(offsets[:]))
+            return picked
 
-        def multiply(bank, stationary, columns, moving):
+        def quantise(values, name):
+            width = values.shape[1] // PACK
+            words = held.tile([P, width], U32, name=name + "_words", align_bytes=64)
+            scales = held.tile([P, width], U8, name=name + "_scales", align_bytes=64)
+            nc.vector.quantize_mx(out=words[:].bitcast(FP8X4), scales=scales[:], in_=values)
+            return words, scales
+
+        def multiply(target, stationary, columns, moving):
             nc.tensor.matmul_mx(
-                out=bank,
+                out=target,
                 lhsT=stationary[0][:, columns].bitcast(FP8X4),
                 lhsT_scale=stationary[1][:, columns],
                 rhs=moving[0][:].bitcast(FP8X4),
@@ -55,10 +68,10 @@ def tile_picked_interl_none_p_kernel(
                 stop=True,
             )
 
-        def project(weights, columns, tokens, name, tag):
+        def project(weights, columns, tokens, name, tag=None):
             bank = psum.tile([P, S], F32, name="bank")
             multiply(bank[:], weights, columns, tokens)
-            values = held.tile([P, S], F32, name=name, tag=tag, align_bytes=64)
+            values = held.tile([P, S], F32, name=name, tag=tag or name, align_bytes=64)
             nc.scalar.copy(values[:], bank[:])
             return values
 
@@ -83,102 +96,95 @@ def tile_picked_interl_none_p_kernel(
         table_scales = held.tile([P, T], U8, name="table_scales")
         nc.vector.memset(table_scales[:].bitcast(I32), 0)
         for rows in quadrants:
-            nc.vector.tensor_copy(table_scales[rows, :].bitcast(I32), scale_rows[rows, :].bitcast(I32))
-
-        def gather(table, offsets, dtype, name):
-            picked = held.tile([P, S], dtype, name=name, align_bytes=64)
-            nc.vector.tensor_copy(picked[:], table[:].indirect(offsets[:]))
-            return picked
-
+            nc.vector.tensor_copy(
+                table_scales[rows, :].bitcast(I32), scale_rows[rows, :].bitcast(I32)
+            )
         text_scales = gather(table_scales, text_list, U8, "text_scales")
         image_scales = gather(table_scales, image_list, U8, "image_scales")
 
-        def quantise_plane(raw, t, name):
-            rounded = held.tile([P, P * PACK], BF16, name=name + "_bf", align_bytes=64)
+        w1_mx = {}
+        for t in PLANES:
+            w1_bf = held.tile([P, P * PACK], BF16, name="w1_bf%d" % t, align_bytes=64)
             nc.scalar.copy(
-                rounded[:].rearrange("p (m j) -> p m j", j=PACK),
-                raw[:].rearrange("p j (m t) -> p t m j", t=PACK)[:, t],
+                w1_bf[:].rearrange("p (m j) -> p m j", j=PACK),
+                w1_raw[:].rearrange("p j (m t) -> p t m j", t=PACK)[:, t],
             )
-            return quantise(rounded[:], name)
+            w1_mx[t] = quantise(w1_bf[:], "w1_%d" % t)
 
-        w1_mx = {t: quantise_plane(w1_raw, t, "w1_%d" % t) for t in PLANES}
         text = (gather(table_words, text_list, U32, "text_words"), text_scales)
         image = (gather(table_words, image_list, U32, "image_words"), image_scales)
-        y = {t: project(w1_mx[t], slice(0, P), text, "y%d" % t, "y%d" % t) for t in PLANES[:-1]}
-        z = {}
 
-        def place_text(t, tag):
-            z[t] = held.tile([P, U], F32, name="z%d" % t, tag=tag, align_bytes=64)
+        y, z = {}, {}
+
+        def project_text(t, tag=None):
+            y[t] = project(w1_mx[t], block(0), text, "y%d" % t, tag)
+
+        def place_text(t):
+            z[t] = held.tile([P, U], F32, name="z%d" % t, align_bytes=64)
             nc.vector.tensor_copy(z[t][:].indirect(text_places[:]), y[t][:])
 
-        place_text(PLANES[0], "z_first")
-        place_text(PLANES[1], "z_second")
+        for t in (FIRST, SECOND):
+            project_text(t)
+        for t in (FIRST, SECOND):
+            place_text(t)
 
-        w2_mx = {t: quantise_plane(w2_raw, t, "w2_%d" % t) for t in PLANES}
-        place_text(PLANES[2], "w2_%d_bf" % PLANES[0])
-        t = PLANES[-1]
-        y[t] = project(w1_mx[t], slice(0, P), text, "y%d" % t, "y%d" % t)
-        e = {}
-        t = PLANES[0]
-        e[t] = project(w2_mx[t], slice(0, P), image, "e%d" % t, "e%d" % t)
+        w2_bf = held.tile([P, PACK * H], BF16, name="w2_bf", align_bytes=64)
+        nc.scalar.copy(
+            w2_bf[:].rearrange("p (t m j) -> p t m j", t=PACK, j=PACK),
+            w2_raw[:].rearrange("p j (m t) -> p t m j", t=PACK),
+        )
+        w2_mx = quantise(w2_bf[:], "w2")
+
+        project_text(THIRD, tag="w2_raw")
+        place_text(THIRD)
 
         starts = [sum(CHUNKS[:i]) for i in range(len(CHUNKS))]
-        chunks = [slice(c, c + width) for c, width in zip(starts, CHUNKS)]
+        chunks = [slice(start, start + width) for start, width in zip(starts, CHUNKS)]
+        widest = len(CHUNKS) - 1
         z_bf = [
             held.tile([P, width, PACK], BF16, name="z_bf%d" % i, align_bytes=64)
             for i, width in enumerate(CHUNKS)
         ]
 
-        def plane(t):
-            return slice(P * t, P * (t + 1))
+        e = {t: project(w2_mx, block(t), image, "e%d" % t) for t in (FIRST, SECOND, THIRD)}
 
-
-        w3_bf = held.tile([P, PACK * N], BF16, name="w3_bf", tag="w3_bf", align_bytes=64)
+        w3_bf = held.tile([P, PACK * N], BF16, name="w3_bf", align_bytes=64)
         for m in range(N // P):
+            if m == N // P - 1:
+                project_text(LAST)
             nc.scalar.copy(
-                w3_bf[:].rearrange("p (c j) -> p c j", j=PACK)[:, plane(m), :],
-                w3_raw[:].rearrange("p j c -> p c j")[:, plane(m), :],
+                w3_bf[:].rearrange("p (c j) -> p c j", j=PACK)[:, block(m), :],
+                w3_raw[:].rearrange("p j c -> p c j")[:, block(m), :],
             )
 
-        for t in PLANES[1:3]:
-            e[t] = project(w2_mx[t], slice(0, P), image, "e%d" % t, "e%d" % t)
-        for t in PLANES[:-1]:
+        for t in (FIRST, SECOND, THIRD):
             nc.vector.tensor_copy(z[t][:].indirect(image_places[:]), e[t][:])
             for i, columns in enumerate(chunks):
-                if t == PLANES[2] and i == 3:
-                    e_last = project(w2_mx[PLANES[3]], plane(0), image, "e_last", "z_second")
+                if t == THIRD and i == widest:
+                    e[LAST] = project(w2_mx, block(LAST), image, "e%d" % LAST, tag="z%d" % SECOND)
                 nc.scalar.copy(z_bf[i][:, :, t], z[t][:, columns])
-        t = PLANES[-1]
-        place_text(t, "e%d" % PLANES[2])
-        w3_mx = quantise(w3_bf[:], "w3", "y%d" % t)
-        nc.vector.tensor_copy(z[t][:].indirect(image_places[:]), e_last[:])
+        place_text(LAST)
+        w3_mx = quantise(w3_bf[:], "w3")
+        nc.vector.tensor_copy(z[LAST][:].indirect(image_places[:]), e[LAST][:])
 
         z_mx = []
         for i, columns in enumerate(chunks):
-            if i == len(chunks) - 1:
-                nc.scalar.copy(z_bf[i][:, :, t], z[t][:, columns])
+            if i == widest:
+                nc.scalar.copy(z_bf[i][:, :, LAST], z[LAST][:, columns])
             else:
-                nc.vector.tensor_copy(z_bf[i][:, :, t], z[t][:, columns])
-            z_mx.append(quantise(z_bf[i][:].rearrange("p c j -> p (c j)"), "z%d" % i))
+                nc.vector.tensor_copy(z_bf[i][:, :, LAST], z[LAST][:, columns])
+            z_mx.append(quantise(z_bf[i][:].rearrange("p c j -> p (c j)"), "z%d_mx" % i))
 
-        out_rows = out.rearrange("(m p) w -> p m w", p=P)
-        for half in range(2):
-            bank = psum.tile([P, 2, CHUNKS[0]], F32, name="bank")
-            for m in range(2):
-                multiply(bank[:, m, :], w3_mx, plane(2 * half + m), z_mx[0])
-            result = held.tile([P, 2, CHUNKS[0]], F32, name="result_a%d" % half)
-            nc.scalar.copy(result[:], bank[:])
-            nc.sync.dma_start(out_rows[:, 2 * half : 2 * half + 2, chunks[0]], result[:])
-        for group in ((1, 2), (3,)):
-            first, last = chunks[group[0]].start, chunks[group[-1]].stop
+        for group in STORES:
+            first, end = chunks[group[0]].start, chunks[group[-1]].stop
             for m in range(N // P):
-                bank = psum.tile([P, last - first], F32, name="bank")
+                bank = psum.tile([P, end - first], F32, name="bank")
                 for i in group:
                     within = slice(chunks[i].start - first, chunks[i].stop - first)
-                    multiply(bank[:, within], w3_mx, plane(m), z_mx[i])
-                result = held.tile([P, last - first], F32, name="result%d_%d" % (first, m))
-                if m % 2:
+                    multiply(bank[:, within], w3_mx, block(m), z_mx[i])
+                result = held.tile([P, end - first], F32, name="result%d_%d" % (first, m))
+                if group != STORES[0] and m % 2 == 1:
                     nc.vector.tensor_copy(result[:], bank[:])
                 else:
                     nc.scalar.copy(result[:], bank[:])
-                nc.sync.dma_start(out[plane(m), first:last], result[:])
+                nc.sync.dma_start(out[block(m), first:end], result[:])

@@ -15,16 +15,18 @@ FP8X4 = mybir.dt.float8_e4m3fn_x4
 
 P = 128
 PACK = 4
+BLOCK_ROWS = 8
 PSUM_BANKS = 8
 
-FIRST, SECOND, THIRD, LAST = PLANES = (1, 2, 3, 0)
+FIRST, SECOND, THIRD, LAST = PLANES = (3, 1, 2, 0)
+W3_LATE = 16
 
 CHUNKS = (128, 128, 256, 512)
 STORES = ((0,), (1, 2), (3,))
 
 
-def block(index):
-    return slice(P * index, P * (index + 1))
+def block(index, width=P):
+    return slice(width * index, width * (index + 1))
 
 
 def tile_picked_interl_none_p_kernel(
@@ -57,23 +59,31 @@ def tile_picked_interl_none_p_kernel(
             nc.vector.quantize_mx(out=words[:].bitcast(FP8X4), scales=scales[:], in_=values)
             return words, scales
 
-        def multiply(target, stationary, columns, moving):
+        def multiply(target, stationary, columns, moving, tokens=slice(None)):
             nc.tensor.matmul_mx(
                 out=target,
                 lhsT=stationary[0][:, columns].bitcast(FP8X4),
                 lhsT_scale=stationary[1][:, columns],
-                rhs=moving[0][:].bitcast(FP8X4),
-                rhs_scale=moving[1][:],
+                rhs=moving[0][:, tokens].bitcast(FP8X4),
+                rhs_scale=moving[1][:, tokens],
                 start=True,
                 stop=True,
             )
 
-        def project(weights, columns, tokens, name, tag=None):
-            bank = psum.tile([P, S], F32, name="bank")
-            multiply(bank[:], weights, columns, tokens)
+        def project(weights, columns, moving, name, tag=None, parts=1):
             values = held.tile([P, S], F32, name=name, tag=tag or name, align_bytes=64)
-            nc.scalar.copy(values[:], bank[:])
+            for part in range(parts):
+                tokens = block(part, S // parts)
+                bank = psum.tile([P, S // parts], F32, name="bank")
+                multiply(bank[:], weights, columns, moving, tokens)
+                nc.scalar.copy(values[:, tokens], bank[:])
             return values
+
+        def round_plane(target, raw, t):
+            nc.scalar.copy(
+                target.rearrange("p (b r j) -> p b r j", r=BLOCK_ROWS, j=PACK),
+                raw[:].rearrange("p j (b t r) -> p t b r j", t=PACK, r=BLOCK_ROWS)[:, t],
+            )
 
         scale_rows = held.tile([P, T], U8, name="scale_rows")
         quadrants = [slice(32 * q, 32 * q + 4) for q in range(4)]
@@ -91,7 +101,12 @@ def tile_picked_interl_none_p_kernel(
         text_places = load_list(la, "text_places")
         w2_raw = load_weight(w2, "w2_raw")
         image_places = load_list(lb, "image_places")
-        w3_raw = load_weight(w3, "w3_raw")
+        w3_raw = held.tile([P, PACK, N], F32, name="w3_raw", align_bytes=64)
+        for t in range(PACK):
+            nc.sync.dma_start(
+                w3_raw[:, t, :],
+                w3.rearrange("(b t r) c -> t b r c", t=PACK, r=BLOCK_ROWS)[t],
+            )
 
         table_scales = held.tile([P, T], U8, name="table_scales")
         nc.vector.memset(table_scales[:].bitcast(I32), 0)
@@ -105,34 +120,38 @@ def tile_picked_interl_none_p_kernel(
         w1_mx = {}
         for t in PLANES:
             w1_bf = held.tile([P, P * PACK], BF16, name="w1_bf%d" % t, align_bytes=64)
-            nc.scalar.copy(
-                w1_bf[:].rearrange("p (m j) -> p m j", j=PACK),
-                w1_raw[:].rearrange("p j (m t) -> p t m j", t=PACK)[:, t],
-            )
+            round_plane(w1_bf[:], w1_raw, t)
             w1_mx[t] = quantise(w1_bf[:], "w1_%d" % t)
 
-        text = (gather(table_words, text_list, U32, "text_words"), text_scales)
+        text_words = held.tile([P, S], U32, name="text_words", align_bytes=64)
+        for half in range(2):
+            nc.vector.tensor_copy(
+                text_words[:, block(half, S // 2)],
+                table_words[:].indirect(text_list[:, block(half, S // 32)]),
+            )
+        text = (text_words, text_scales)
         image = (gather(table_words, image_list, U32, "image_words"), image_scales)
 
-        y, z = {}, {}
+        y = {}
+        z = {
+            t: held.tile([P, U if t % 2 else 2 * U], F32, name="z%d" % t, align_bytes=64)
+            for t in PLANES
+        }
 
-        def project_text(t, tag=None):
-            y[t] = project(w1_mx[t], block(0), text, "y%d" % t, tag)
+        def project_text(t, tag=None, parts=1):
+            y[t] = project(w1_mx[t], block(0), text, "y%d" % t, tag, parts)
 
         def place_text(t):
-            z[t] = held.tile([P, U], F32, name="z%d" % t, align_bytes=64)
             nc.vector.tensor_copy(z[t][:].indirect(text_places[:]), y[t][:])
 
-        for t in (FIRST, SECOND):
-            project_text(t)
+        project_text(FIRST, parts=2)
+        project_text(SECOND)
         for t in (FIRST, SECOND):
             place_text(t)
 
         w2_bf = held.tile([P, PACK * H], BF16, name="w2_bf", align_bytes=64)
-        nc.scalar.copy(
-            w2_bf[:].rearrange("p (t m j) -> p t m j", t=PACK, j=PACK),
-            w2_raw[:].rearrange("p j (m t) -> p t m j", t=PACK),
-        )
+        for t in PLANES:
+            round_plane(w2_bf[:, block(t, P * PACK)], w2_raw, t)
         w2_mx = quantise(w2_bf[:], "w2")
 
         project_text(THIRD, tag="w2_raw")
@@ -149,30 +168,43 @@ def tile_picked_interl_none_p_kernel(
         e = {t: project(w2_mx, block(t), image, "e%d" % t) for t in (FIRST, SECOND, THIRD)}
 
         w3_bf = held.tile([P, PACK * N], BF16, name="w3_bf", align_bytes=64)
-        for m in range(N // P):
-            if m == N // P - 1:
-                project_text(LAST)
+
+        def round_w3(columns):
             nc.scalar.copy(
-                w3_bf[:].rearrange("p (c j) -> p c j", j=PACK)[:, block(m), :],
-                w3_raw[:].rearrange("p j c -> p c j")[:, block(m), :],
+                w3_bf[:].rearrange("p (c j) -> p c j", j=PACK)[:, columns, :],
+                w3_raw[:].rearrange("p j c -> p c j")[:, columns, :],
             )
 
-        for t in (FIRST, SECOND, THIRD):
+        def place_image(t):
             nc.vector.tensor_copy(z[t][:].indirect(image_places[:]), e[t][:])
-            for i, columns in enumerate(chunks):
-                if t == THIRD and i == widest:
-                    e[LAST] = project(w2_mx, block(LAST), image, "e%d" % LAST, tag="z%d" % SECOND)
-                nc.scalar.copy(z_bf[i][:, :, t], z[t][:, columns])
+
+        def round_pair(engine_copy, t, i):
+            engine_copy(
+                z_bf[i][:, :, t : t + 2],
+                z[t][:].rearrange("p (s c) -> p c s", s=2)[:, chunks[i], :],
+            )
+
+        project_text(LAST)
+        round_w3(slice(0, N // 2))
+        round_w3(slice(N // 2, N - W3_LATE))
+
+        place_image(FIRST)
+        nc.scalar.copy(z[THIRD][:, U:], z[FIRST][:])
+        place_image(SECOND)
+        nc.scalar.copy(z[LAST][:, U:], z[SECOND][:])
+        round_w3(slice(N - W3_LATE, N))
+        place_image(THIRD)
+        for i in range(widest):
+            round_pair(nc.scalar.copy, THIRD, i)
+        e[LAST] = project(w2_mx, block(LAST), image, "e%d" % LAST, tag="z%d" % SECOND)
+        round_pair(nc.scalar.copy, THIRD, widest)
         place_text(LAST)
         w3_mx = quantise(w3_bf[:], "w3")
-        nc.vector.tensor_copy(z[LAST][:].indirect(image_places[:]), e[LAST][:])
+        place_image(LAST)
 
         z_mx = []
-        for i, columns in enumerate(chunks):
-            if i == widest:
-                nc.scalar.copy(z_bf[i][:, :, LAST], z[LAST][:, columns])
-            else:
-                nc.vector.tensor_copy(z_bf[i][:, :, LAST], z[LAST][:, columns])
+        for i in range(len(CHUNKS)):
+            round_pair(nc.scalar.copy if i == widest else nc.vector.tensor_copy, LAST, i)
             z_mx.append(quantise(z_bf[i][:].rearrange("p c j -> p (c j)"), "z%d_mx" % i))
 
         for group in STORES:

@@ -21,8 +21,8 @@ PSUM_BANKS = 8
 FIRST, SECOND, THIRD, LAST = PLANES = (3, 1, 2, 0)
 W3_LATE = 16
 
-CHUNKS = (128, 128, 256, 512)
-STORES = ((0,), (1, 2), (3,))
+CHUNKS = (256, 256, 512)
+STORES = ((0, 1), (2,))
 
 
 def block(index, width=P):
@@ -88,7 +88,7 @@ def tile_picked_interl_none_p_kernel(
         scale_rows = held.tile([P, T], U8, name="scale_rows")
         quadrants = [slice(32 * q, 32 * q + 4) for q in range(4)]
         for q, rows in enumerate(quadrants):
-            nc.sync.dma_start(
+            (nc.sync, nc.scalar)[q % 2].dma_start(
                 scale_rows[rows, :].bitcast(I32), x_scales[0, 4 * q : 4 * q + 4, :].bitcast(I32)
             )
         text_list = load_list(offs, "text_list")
@@ -167,56 +167,65 @@ def tile_picked_interl_none_p_kernel(
 
         e = {t: project(w2_mx, block(t), image, "e%d" % t) for t in (FIRST, SECOND, THIRD)}
 
-        w3_bf = held.tile([P, PACK * N], BF16, name="w3_bf", align_bytes=64)
+        w3_bf = [
+            held.tile([P, N // 2, PACK], BF16, name="w3_bf%d" % half, align_bytes=64)
+            for half in range(2)
+        ]
 
-        def round_w3(columns):
+        def round_w3(half, first, end):
             nc.scalar.copy(
-                w3_bf[:].rearrange("p (c j) -> p c j", j=PACK)[:, columns, :],
-                w3_raw[:].rearrange("p j c -> p c j")[:, columns, :],
+                w3_bf[half][:, first:end, :],
+                w3_raw[:, :, block(half, N // 2)].rearrange("p j c -> p c j")[:, first:end, :],
             )
 
         def place_image(t):
             nc.vector.tensor_copy(z[t][:].indirect(image_places[:]), e[t][:])
 
-        def round_pair(engine_copy, t, i):
+        def round_pair(engine_copy, t, i, first=0, end=None):
+            end = CHUNKS[i] if end is None else end
             engine_copy(
-                z_bf[i][:, :, t : t + 2],
-                z[t][:].rearrange("p (s c) -> p c s", s=2)[:, chunks[i], :],
+                z_bf[i][:, first:end, t : t + 2],
+                z[t][:].rearrange("p (s c) -> p c s", s=2)[:, starts[i] + first : starts[i] + end, :],
             )
 
         project_text(LAST)
-        round_w3(slice(0, N // 2))
-        round_w3(slice(N // 2, N - W3_LATE))
+        for half in range(2):
+            round_w3(half, 0, N // 2 - W3_LATE)
 
         place_image(FIRST)
         nc.scalar.copy(z[THIRD][:, U:], z[FIRST][:])
         place_image(SECOND)
         nc.scalar.copy(z[LAST][:, U:], z[SECOND][:])
-        round_w3(slice(N - W3_LATE, N))
+        round_w3(0, N // 2 - W3_LATE, N // 2)
         place_image(THIRD)
-        for i in range(widest):
+        for i in (2, 0):
             round_pair(nc.scalar.copy, THIRD, i)
         e[LAST] = project(w2_mx, block(LAST), image, "e%d" % LAST, tag="z%d" % SECOND)
-        round_pair(nc.scalar.copy, THIRD, widest)
+        round_w3(1, N // 2 - W3_LATE, N // 2)
+        round_pair(nc.scalar.copy, THIRD, 1)
         place_text(LAST)
-        w3_mx = quantise(w3_bf[:], "w3")
+        w3_mx = [quantise(w3_bf[0][:].rearrange("p c j -> p (c j)"), "w3_0")]
         place_image(LAST)
+        w3_mx.append(quantise(w3_bf[1][:].rearrange("p c j -> p (c j)"), "w3_1"))
 
-        z_mx = []
-        for i in range(len(CHUNKS)):
-            round_pair(nc.scalar.copy if i == widest else nc.vector.tensor_copy, LAST, i)
-            z_mx.append(quantise(z_bf[i][:].rearrange("p c j -> p (c j)"), "z%d_mx" % i))
 
+        round_pair(nc.vector.tensor_copy, LAST, 0)
+        round_pair(nc.scalar.copy, LAST, 1)
+        round_pair(nc.vector.tensor_copy, LAST, 2, end=P)
+        round_pair(nc.scalar.copy, LAST, 2, first=P)
+        z_mx = [
+            quantise(z_bf[i][:].rearrange("p c j -> p (c j)"), "z%d_mx" % i)
+            for i in range(len(CHUNKS))
+        ]
+
+        copies_out = (nc.vector.tensor_copy, nc.scalar.copy)
         for group in STORES:
             first, end = chunks[group[0]].start, chunks[group[-1]].stop
             for m in range(N // P):
-                bank = psum.tile([P, end - first], F32, name="bank")
-                for i in group:
-                    within = slice(chunks[i].start - first, chunks[i].stop - first)
-                    multiply(bank[:, within], w3_mx, block(m), z_mx[i])
                 result = held.tile([P, end - first], F32, name="result%d_%d" % (first, m))
-                if group != STORES[0] and m % 2 == 1:
-                    nc.vector.tensor_copy(result[:], bank[:])
-                else:
-                    nc.scalar.copy(result[:], bank[:])
+                for i in group:
+                    bank = psum.tile([P, CHUNKS[i]], F32, name="bank")
+                    multiply(bank[:], w3_mx[m // 2], block(m % 2), z_mx[i])
+                    copy_out = copies_out[i if len(group) > 1 else m % 2]
+                    copy_out(result[:, chunks[i].start - first : chunks[i].stop - first], bank[:])
                 nc.sync.dma_start(out[block(m), first:end], result[:])

@@ -21,8 +21,8 @@ PSUM_BANKS = 8
 FIRST, SECOND, THIRD, LAST = PLANES = (3, 1, 2, 0)
 W3_LATE = 16
 
-CHUNKS = (256, 256, 512)
-STORES = ((0, 1), (2,))
+CHUNKS = (128, 128, 128, 128, 512)
+HALF = U // 2
 
 
 def block(index, width=P):
@@ -158,8 +158,6 @@ def tile_picked_interl_none_p_kernel(
         place_text(THIRD)
 
         starts = [sum(CHUNKS[:i]) for i in range(len(CHUNKS))]
-        chunks = [slice(start, start + width) for start, width in zip(starts, CHUNKS)]
-        widest = len(CHUNKS) - 1
         z_bf = [
             held.tile([P, width, PACK], BF16, name="z_bf%d" % i, align_bytes=64)
             for i, width in enumerate(CHUNKS)
@@ -198,34 +196,63 @@ def tile_picked_interl_none_p_kernel(
         nc.scalar.copy(z[LAST][:, U:], z[SECOND][:])
         round_w3(0, N // 2 - W3_LATE, N // 2)
         place_image(THIRD)
-        for i in (2, 0):
+        for i in (4, 0, 1):
             round_pair(nc.scalar.copy, THIRD, i)
         e[LAST] = project(w2_mx, block(LAST), image, "e%d" % LAST, tag="z%d" % SECOND)
         round_w3(1, N // 2 - W3_LATE, N // 2)
-        round_pair(nc.scalar.copy, THIRD, 1)
+        for i in (2, 3):
+            round_pair(nc.scalar.copy, THIRD, i)
         place_text(LAST)
         w3_mx = [quantise(w3_bf[0][:].rearrange("p c j -> p (c j)"), "w3_0")]
         place_image(LAST)
         w3_mx.append(quantise(w3_bf[1][:].rearrange("p c j -> p (c j)"), "w3_1"))
 
 
-        round_pair(nc.vector.tensor_copy, LAST, 0)
-        round_pair(nc.scalar.copy, LAST, 1)
-        round_pair(nc.vector.tensor_copy, LAST, 2, end=P)
-        round_pair(nc.scalar.copy, LAST, 2, first=P)
-        z_mx = [
-            quantise(z_bf[i][:].rearrange("p c j -> p (c j)"), "z%d_mx" % i)
-            for i in range(len(CHUNKS))
+        halves = [
+            (
+                held.tile([P, HALF], U32, name="z_words%d" % h, align_bytes=64),
+                held.tile([P, HALF], U8, name="z_scales%d" % h, align_bytes=64),
+            )
+            for h in range(2)
         ]
 
-        copies_out = (nc.vector.tensor_copy, nc.scalar.copy)
-        for group in STORES:
-            first, end = chunks[group[0]].start, chunks[group[-1]].stop
-            for m in range(N // P):
-                result = held.tile([P, end - first], F32, name="result%d_%d" % (first, m))
-                for i in group:
-                    bank = psum.tile([P, CHUNKS[i]], F32, name="bank")
-                    multiply(bank[:], w3_mx[m // 2], block(m % 2), z_mx[i])
-                    copy_out = copies_out[i if len(group) > 1 else m % 2]
-                    copy_out(result[:, chunks[i].start - first : chunks[i].stop - first], bank[:])
-                nc.sync.dma_start(out[block(m), first:end], result[:])
+        def quantise_chunk(i):
+            words, scales = halves[starts[i] // HALF]
+            columns = slice(starts[i] % HALF, starts[i] % HALF + CHUNKS[i])
+            nc.vector.quantize_mx(
+                out=words[:, columns].bitcast(FP8X4),
+                scales=scales[:, columns],
+                in_=z_bf[i][:].rearrange("p c j -> p (c j)"),
+            )
+
+        results = {
+            (h, m): held.tile([P, HALF], F32, name="result%d_%d" % (h, m))
+            for h in range(2)
+            for m in range(N // P)
+        }
+
+        def produce(h, m, copies):
+            width = HALF // len(copies)
+            for part, copy_out in enumerate(copies):
+                bank = psum.tile([P, width], F32, name="bank")
+                multiply(bank[:], w3_mx[m // 2], block(m % 2), halves[h], block(part, width))
+                copy_out(results[h, m][:, block(part, width)], bank[:])
+            nc.sync.dma_start(out[block(m), block(h, HALF)], results[h, m][:])
+
+        vector, scalar = nc.vector.tensor_copy, nc.scalar.copy
+        round_pair(vector, LAST, 0)
+        round_pair(vector, LAST, 1)
+        round_pair(scalar, LAST, 2)
+        round_pair(scalar, LAST, 3)
+        for i in range(4):
+            quantise_chunk(i)
+        round_pair(scalar, LAST, 4, first=3 * P)
+        produce(0, 0, [scalar] * 4)
+        for part in range(3):
+            round_pair(vector, LAST, 4, first=part * P, end=(part + 1) * P)
+        quantise_chunk(4)
+        produce(0, 1, [scalar] * 2)
+        produce(0, 2, [scalar] * 2)
+        produce(0, 3, [vector, scalar])
+        for m in range(N // P):
+            produce(1, m, [vector, scalar])

@@ -194,11 +194,15 @@ def tile_picked_interl_none_p_kernel(
         nc.scalar.copy(z[THIRD][:, U:], z[FIRST][:])
         place_image(SECOND)
         nc.scalar.copy(z[LAST][:, U:], z[SECOND][:])
+        last_bank = psum.tile([P, S], F32, name="bank")
+        multiply(last_bank[:], w2_mx, block(LAST), image)
+        e[LAST] = held.tile([P, S], F32, name="e_last", tag="z%d" % SECOND, align_bytes=64)
+        nc.scalar.copy(e[LAST][:, W3_LATE:], last_bank[:, W3_LATE:])
         round_w3(0, N // 2 - W3_LATE, N // 2)
         place_image(THIRD)
         for i in (4, 0, 1):
             round_pair(nc.scalar.copy, THIRD, i)
-        e[LAST] = project(w2_mx, block(LAST), image, "e%d" % LAST, tag="z%d" % SECOND)
+        nc.scalar.copy(e[LAST][:, :W3_LATE], last_bank[:, :W3_LATE])
         round_w3(1, N // 2 - W3_LATE, N // 2)
         for i in (2, 3):
             round_pair(nc.scalar.copy, THIRD, i)
@@ -250,8 +254,8 @@ def tile_picked_interl_none_p_kernel(
         produce(0, 0, [scalar] * 4)
         for part in range(3):
             round_pair(vector, LAST, 4, first=part * P, end=(part + 1) * P)
+        produce(0, 1, [vector, scalar])
         quantise_chunk(4)
-        produce(0, 1, [scalar] * 2)
         produce(0, 2, [scalar] * 2)
         produce(0, 3, [vector, scalar])
         for m in range(N // P):

@@ -92,8 +92,8 @@ def tile_picked_interl_none_p_kernel(
                 scale_rows[rows, :].bitcast(I32), x_scales[0, 4 * q : 4 * q + 4, :].bitcast(I32)
             )
         text_list = load_list(offs, "text_list")
-        image_list = load_list(img, "image_list")
         w1_raw = load_weight(w1, "w1_raw")
+        image_list = load_list(img, "image_list")
         table_words = held.tile([P, T], U32, name="table_words")
         nc.sync.dma_start(
             table_words[:].bitcast(I32), x_words[0].rearrange("p c r -> p (c r)").bitcast(I32)
@@ -165,16 +165,21 @@ def tile_picked_interl_none_p_kernel(
 
         e = {t: project(w2_mx, block(t), image, "e%d" % t) for t in (FIRST, SECOND, THIRD)}
 
+        w3_parts = (slice(0, 2 * P), block(2), block(3))
         w3_bf = [
-            held.tile([P, N // 2, PACK], BF16, name="w3_bf%d" % half, align_bytes=64)
-            for half in range(2)
+            held.tile([P, part.stop - part.start, PACK], BF16, name="w3_bf%d" % i, align_bytes=64)
+            for i, part in enumerate(w3_parts)
         ]
 
-        def round_w3(half, first, end):
+        def round_w3(i, late):
+            columns = slice(0, W3_LATE) if late else slice(W3_LATE, None)
             nc.scalar.copy(
-                w3_bf[half][:, first:end, :],
-                w3_raw[:, :, block(half, N // 2)].rearrange("p j c -> p c j")[:, first:end, :],
+                w3_bf[i][:, columns, :],
+                w3_raw[:, :, w3_parts[i]].rearrange("p j c -> p c j")[:, columns, :],
             )
+
+        def quantise_w3(i):
+            return quantise(w3_bf[i][:].rearrange("p c j -> p (c j)"), "w3_%d" % i)
 
         def place_image(t):
             nc.vector.tensor_copy(z[t][:].indirect(image_places[:]), e[t][:])
@@ -187,8 +192,8 @@ def tile_picked_interl_none_p_kernel(
             )
 
         project_text(LAST)
-        for half in range(2):
-            round_w3(half, 0, N // 2 - W3_LATE)
+        for i in range(3):
+            round_w3(i, False)
 
         place_image(FIRST)
         nc.scalar.copy(z[THIRD][:, U:], z[FIRST][:])
@@ -198,18 +203,18 @@ def tile_picked_interl_none_p_kernel(
         multiply(last_bank[:], w2_mx, block(LAST), image)
         e[LAST] = held.tile([P, S], F32, name="e_last", tag="z%d" % SECOND, align_bytes=64)
         nc.scalar.copy(e[LAST][:, W3_LATE:], last_bank[:, W3_LATE:])
-        round_w3(0, N // 2 - W3_LATE, N // 2)
+        round_w3(0, True)
         place_image(THIRD)
         for i in (4, 0, 1):
             round_pair(nc.scalar.copy, THIRD, i)
         nc.scalar.copy(e[LAST][:, :W3_LATE], last_bank[:, :W3_LATE])
-        round_w3(1, N // 2 - W3_LATE, N // 2)
+        round_w3(1, True)
         for i in (2, 3):
             round_pair(nc.scalar.copy, THIRD, i)
         place_text(LAST)
-        w3_mx = [quantise(w3_bf[0][:].rearrange("p c j -> p (c j)"), "w3_0")]
+        w3_mx = [quantise_w3(0)]
         place_image(LAST)
-        w3_mx.append(quantise(w3_bf[1][:].rearrange("p c j -> p (c j)"), "w3_1"))
+        w3_mx.append(quantise_w3(1))
 
 
         halves = [
@@ -239,17 +244,25 @@ def tile_picked_interl_none_p_kernel(
             width = HALF // len(copies)
             for part, copy_out in enumerate(copies):
                 bank = psum.tile([P, width], F32, name="bank")
-                multiply(bank[:], w3_mx[m // 2], block(m % 2), halves[h], block(part, width))
+                weights, columns = w3_mx[max(m - 1, 0)], block(m if m < 2 else 0)
+                multiply(bank[:], weights, columns, halves[h], block(part, width))
                 copy_out(results[h, m][:, block(part, width)], bank[:])
             nc.sync.dma_start(out[block(m), block(h, HALF)], results[h, m][:])
+
+        idle = psum.tile([P, S], F32, name="bank")
+        multiply(idle[:], w3_mx[1], block(0), text)
+        idle = psum.tile([P, P], F32, name="bank")
+        multiply(idle[:], w3_mx[1], block(0), text, block(0))
 
         vector, scalar = nc.vector.tensor_copy, nc.scalar.copy
         round_pair(vector, LAST, 0)
         round_pair(vector, LAST, 1)
         round_pair(scalar, LAST, 2)
         round_pair(scalar, LAST, 3)
+        round_w3(2, True)
         for i in range(4):
             quantise_chunk(i)
+        w3_mx.append(quantise_w3(2))
         round_pair(scalar, LAST, 4, first=3 * P)
         produce(0, 0, [scalar] * 4)
         for part in range(3):

@@ -256,17 +256,17 @@ def tile_picked_interl_none_p_kernel(
 
         vector, scalar = nc.vector.tensor_copy, nc.scalar.copy
         round_pair(vector, LAST, 0)
-        round_pair(vector, LAST, 1)
-        round_pair(scalar, LAST, 2)
+        round_pair(scalar, LAST, 1)
+        round_pair(vector, LAST, 2)
         round_pair(scalar, LAST, 3)
         round_w3(2, True)
         for i in range(4):
             quantise_chunk(i)
         w3_mx.append(quantise_w3(2))
-        round_pair(scalar, LAST, 4, first=3 * P)
+        round_pair(scalar, LAST, 4, first=HALF - 64)
         produce(0, 0, [scalar] * 4)
-        for part in range(3):
-            round_pair(vector, LAST, 4, first=part * P, end=(part + 1) * P)
+        for first, end in ((0, P), (P, 2 * P), (2 * P, HALF - 64)):
+            round_pair(vector, LAST, 4, first=first, end=end)
         produce(0, 1, [vector, scalar])
         quantise_chunk(4)
         produce(0, 2, [scalar] * 2)

@@ -19,10 +19,13 @@ BLOCK_ROWS = 8
 PSUM_BANKS = 8
 
 FIRST, SECOND, THIRD, LAST = PLANES = (3, 1, 2, 0)
-W3_LATE = 16
 
-CHUNKS = (128, 128, 128, 128, 512)
+LATE = 16
+
 HALF = U // 2
+CHUNKS = (P, P, P, P, HALF)
+WIDE = len(CHUNKS) - 1
+SCALAR_SHARE = 64
 
 
 def block(index, width=P):
@@ -33,6 +36,7 @@ def tile_picked_interl_none_p_kernel(
     tc, x_words, x_scales, w1, w2, w3, offs, img, la, lb, out
 ):
     nc = tc.nc
+    vector_copy, scalar_copy = nc.vector.tensor_copy, nc.scalar.copy
     with ExitStack() as ctx:
         held = ctx.enter_context(tc.tile_pool(name="held", bufs=1))
         psum = ctx.enter_context(tc.psum_pool(name="psum", bufs=PSUM_BANKS))
@@ -49,15 +53,23 @@ def tile_picked_interl_none_p_kernel(
 
         def gather(table, offsets, dtype, name):
             picked = held.tile([P, S], dtype, name=name, align_bytes=64)
-            nc.vector.tensor_copy(picked[:], table[:].indirect(offsets[:]))
+            vector_copy(picked[:], table[:].indirect(offsets[:]))
             return picked
 
-        def quantise(values, name):
-            width = values.shape[1] // PACK
+        def mx_tiles(width, name):
             words = held.tile([P, width], U32, name=name + "_words", align_bytes=64)
             scales = held.tile([P, width], U8, name=name + "_scales", align_bytes=64)
-            nc.vector.quantize_mx(out=words[:].bitcast(FP8X4), scales=scales[:], in_=values)
             return words, scales
+
+        def quantise_into(target, columns, values):
+            nc.vector.quantize_mx(
+                out=target[0][:, columns].bitcast(FP8X4), scales=target[1][:, columns], in_=values
+            )
+
+        def quantise(values, name):
+            target = mx_tiles(values.shape[1] // PACK, name)
+            quantise_into(target, slice(None), values)
+            return target
 
         def multiply(target, stationary, columns, moving, tokens=slice(None)):
             nc.tensor.matmul_mx(
@@ -76,11 +88,11 @@ def tile_picked_interl_none_p_kernel(
                 tokens = block(part, S // parts)
                 bank = psum.tile([P, S // parts], F32, name="bank")
                 multiply(bank[:], weights, columns, moving, tokens)
-                nc.scalar.copy(values[:, tokens], bank[:])
+                scalar_copy(values[:, tokens], bank[:])
             return values
 
         def round_plane(target, raw, t):
-            nc.scalar.copy(
+            scalar_copy(
                 target.rearrange("p (b r j) -> p b r j", r=BLOCK_ROWS, j=PACK),
                 raw[:].rearrange("p j (b t r) -> p t b r j", t=PACK, r=BLOCK_ROWS)[:, t],
             )
@@ -111,9 +123,7 @@ def tile_picked_interl_none_p_kernel(
         table_scales = held.tile([P, T], U8, name="table_scales")
         nc.vector.memset(table_scales[:].bitcast(I32), 0)
         for rows in quadrants:
-            nc.vector.tensor_copy(
-                table_scales[rows, :].bitcast(I32), scale_rows[rows, :].bitcast(I32)
-            )
+            vector_copy(table_scales[rows, :].bitcast(I32), scale_rows[rows, :].bitcast(I32))
         text_scales = gather(table_scales, text_list, U8, "text_scales")
         image_scales = gather(table_scales, image_list, U8, "image_scales")
 
@@ -125,7 +135,7 @@ def tile_picked_interl_none_p_kernel(
 
         text_words = held.tile([P, S], U32, name="text_words", align_bytes=64)
         for half in range(2):
-            nc.vector.tensor_copy(
+            vector_copy(
                 text_words[:, block(half, S // 2)],
                 table_words[:].indirect(text_list[:, block(half, S // 32)]),
             )
@@ -142,7 +152,7 @@ def tile_picked_interl_none_p_kernel(
             y[t] = project(w1_mx[t], block(0), text, "y%d" % t, tag, parts)
 
         def place_text(t):
-            nc.vector.tensor_copy(z[t][:].indirect(text_places[:]), y[t][:])
+            vector_copy(z[t][:].indirect(text_places[:]), y[t][:])
 
         project_text(FIRST, parts=2)
         project_text(SECOND)
@@ -165,111 +175,86 @@ def tile_picked_interl_none_p_kernel(
 
         e = {t: project(w2_mx, block(t), image, "e%d" % t) for t in (FIRST, SECOND, THIRD)}
 
-        w3_parts = (slice(0, 2 * P), block(2), block(3))
         w3_bf = [
-            held.tile([P, part.stop - part.start, PACK], BF16, name="w3_bf%d" % i, align_bytes=64)
-            for i, part in enumerate(w3_parts)
+            held.tile([P, N // 2, PACK], BF16, name="w3_bf%d" % half, align_bytes=64)
+            for half in range(2)
         ]
+        early, late = slice(LATE, None), slice(0, LATE)
 
-        def round_w3(i, late):
-            columns = slice(0, W3_LATE) if late else slice(W3_LATE, None)
-            nc.scalar.copy(
-                w3_bf[i][:, columns, :],
-                w3_raw[:, :, w3_parts[i]].rearrange("p j c -> p c j")[:, columns, :],
+        def round_w3(half, columns):
+            scalar_copy(
+                w3_bf[half][:, columns, :],
+                w3_raw[:, :, block(half, N // 2)].rearrange("p t c -> p c t")[:, columns, :],
             )
 
-        def quantise_w3(i):
-            return quantise(w3_bf[i][:].rearrange("p c j -> p (c j)"), "w3_%d" % i)
+        def quantise_w3(half):
+            return quantise(w3_bf[half][:].rearrange("p c t -> p (c t)"), "w3_%d" % half)
 
         def place_image(t):
-            nc.vector.tensor_copy(z[t][:].indirect(image_places[:]), e[t][:])
+            vector_copy(z[t][:].indirect(image_places[:]), e[t][:])
 
-        def round_pair(engine_copy, t, i, first=0, end=None):
+        def round_pair(copy, t, i, first=0, end=None):
             end = CHUNKS[i] if end is None else end
-            engine_copy(
+            copy(
                 z_bf[i][:, first:end, t : t + 2],
                 z[t][:].rearrange("p (s c) -> p c s", s=2)[:, starts[i] + first : starts[i] + end, :],
             )
 
         project_text(LAST)
-        for i in range(3):
-            round_w3(i, False)
+        for half in range(2):
+            round_w3(half, early)
 
         place_image(FIRST)
-        nc.scalar.copy(z[THIRD][:, U:], z[FIRST][:])
+        scalar_copy(z[THIRD][:, U:], z[FIRST][:])
         place_image(SECOND)
-        nc.scalar.copy(z[LAST][:, U:], z[SECOND][:])
+        scalar_copy(z[LAST][:, U:], z[SECOND][:])
         last_bank = psum.tile([P, S], F32, name="bank")
         multiply(last_bank[:], w2_mx, block(LAST), image)
         e[LAST] = held.tile([P, S], F32, name="e_last", tag="z%d" % SECOND, align_bytes=64)
-        nc.scalar.copy(e[LAST][:, W3_LATE:], last_bank[:, W3_LATE:])
-        round_w3(0, True)
+        scalar_copy(e[LAST][:, early], last_bank[:, early])
+        round_w3(0, late)
         place_image(THIRD)
-        for i in (4, 0, 1):
-            round_pair(nc.scalar.copy, THIRD, i)
-        nc.scalar.copy(e[LAST][:, :W3_LATE], last_bank[:, :W3_LATE])
-        round_w3(1, True)
+        for i in (WIDE, 0, 1):
+            round_pair(scalar_copy, THIRD, i)
+        scalar_copy(e[LAST][:, late], last_bank[:, late])
+        round_w3(1, late)
         for i in (2, 3):
-            round_pair(nc.scalar.copy, THIRD, i)
+            round_pair(scalar_copy, THIRD, i)
         place_text(LAST)
         w3_mx = [quantise_w3(0)]
         place_image(LAST)
         w3_mx.append(quantise_w3(1))
 
-
-        halves = [
-            (
-                held.tile([P, HALF], U32, name="z_words%d" % h, align_bytes=64),
-                held.tile([P, HALF], U8, name="z_scales%d" % h, align_bytes=64),
-            )
-            for h in range(2)
-        ]
+        z_mx = [mx_tiles(HALF, "z_mx%d" % half) for half in range(2)]
 
         def quantise_chunk(i):
-            words, scales = halves[starts[i] // HALF]
-            columns = slice(starts[i] % HALF, starts[i] % HALF + CHUNKS[i])
-            nc.vector.quantize_mx(
-                out=words[:, columns].bitcast(FP8X4),
-                scales=scales[:, columns],
-                in_=z_bf[i][:].rearrange("p c j -> p (c j)"),
+            first = starts[i] % HALF
+            quantise_into(
+                z_mx[starts[i] // HALF],
+                slice(first, first + CHUNKS[i]),
+                z_bf[i][:].rearrange("p c t -> p (c t)"),
             )
 
-        results = {
-            (h, m): held.tile([P, HALF], F32, name="result%d_%d" % (h, m))
-            for h in range(2)
-            for m in range(N // P)
-        }
-
-        def produce(h, m, copies):
+        def produce(half, m, copies):
+            result = held.tile([P, HALF], F32, name="result%d_%d" % (half, m))
             width = HALF // len(copies)
-            for part, copy_out in enumerate(copies):
+            for part, copy in enumerate(copies):
                 bank = psum.tile([P, width], F32, name="bank")
-                weights, columns = w3_mx[max(m - 1, 0)], block(m if m < 2 else 0)
-                multiply(bank[:], weights, columns, halves[h], block(part, width))
-                copy_out(results[h, m][:, block(part, width)], bank[:])
-            nc.sync.dma_start(out[block(m), block(h, HALF)], results[h, m][:])
+                multiply(bank[:], w3_mx[m // 2], block(m % 2), z_mx[half], block(part, width))
+                copy(result[:, block(part, width)], bank[:])
+            nc.sync.dma_start(out[block(m), block(half, HALF)], result[:])
 
-        idle = psum.tile([P, S], F32, name="bank")
-        multiply(idle[:], w3_mx[1], block(0), text)
-        idle = psum.tile([P, P], F32, name="bank")
-        multiply(idle[:], w3_mx[1], block(0), text, block(0))
-
-        vector, scalar = nc.vector.tensor_copy, nc.scalar.copy
-        round_pair(vector, LAST, 0)
-        round_pair(scalar, LAST, 1)
-        round_pair(vector, LAST, 2)
-        round_pair(scalar, LAST, 3)
-        round_w3(2, True)
-        for i in range(4):
+        for i in range(WIDE):
+            round_pair((vector_copy, scalar_copy)[i % 2], LAST, i)
+        for i in range(WIDE):
             quantise_chunk(i)
-        w3_mx.append(quantise_w3(2))
-        round_pair(scalar, LAST, 4, first=HALF - 64)
-        produce(0, 0, [scalar] * 4)
-        for first, end in ((0, P), (P, 2 * P), (2 * P, HALF - 64)):
-            round_pair(vector, LAST, 4, first=first, end=end)
-        produce(0, 1, [vector, scalar])
-        quantise_chunk(4)
-        produce(0, 2, [scalar] * 2)
-        produce(0, 3, [vector, scalar])
+        round_pair(scalar_copy, LAST, WIDE, first=HALF - SCALAR_SHARE)
+        produce(0, 0, [scalar_copy] * WIDE)
+        for first, end in ((0, P), (P, 2 * P), (2 * P, HALF - SCALAR_SHARE)):
+            round_pair(vector_copy, LAST, WIDE, first, end)
+        produce(0, 1, [vector_copy, scalar_copy])
+        quantise_chunk(WIDE)
+        produce(0, 2, [scalar_copy, scalar_copy])
+        produce(0, 3, [vector_copy, scalar_copy])
         for m in range(N // P):
-            produce(1, m, [vector, scalar])
+            produce(1, m, [vector_copy, scalar_copy])

@@ -235,21 +235,23 @@ def tile_picked_interl_none_p_kernel(
                 z_bf[i][:].rearrange("p c t -> p (c t)"),
             )
 
-        def produce(half, m, copies):
+        def produce(half, m, copies, stores=1):
             result = held.tile([P, HALF], F32, name="result%d_%d" % (half, m))
             width = HALF // len(copies)
             for part, copy in enumerate(copies):
                 bank = psum.tile([P, width], F32, name="bank")
                 multiply(bank[:], w3_mx[m // 2], block(m % 2), z_mx[half], block(part, width))
                 copy(result[:, block(part, width)], bank[:])
-            nc.sync.dma_start(out[block(m), block(half, HALF)], result[:])
+            for part in range(stores):
+                columns = block(part, HALF // stores)
+                nc.sync.dma_start(out[block(m), block(half, HALF)][:, columns], result[:, columns])
 
         for i in range(WIDE):
             round_pair((vector_copy, scalar_copy)[i % 2], LAST, i)
         for i in range(WIDE):
             quantise_chunk(i)
         round_pair(scalar_copy, LAST, WIDE, first=HALF - SCALAR_SHARE)
-        produce(0, 0, [scalar_copy] * WIDE)
+        produce(0, 0, [scalar_copy] * WIDE, stores=2)
         for first, end in ((0, P), (P, 2 * P), (2 * P, HALF - SCALAR_SHARE)):
             round_pair(vector_copy, LAST, WIDE, first, end)
         produce(0, 1, [vector_copy, scalar_copy])

@@ -16,12 +16,9 @@ FP8X4 = mybir.dt.float8_e4m3fn_x4
 P = 128
 PACK = 4
 BLOCK_ROWS = 8
+LINE = 4
 PSUM_BANKS = 8
-
-FIRST, SECOND, THIRD, LAST = PLANES = (3, 1, 2, 0)
-
 LATE = 16
-
 HALF = U // 2
 CHUNKS = (P, P, P, P, HALF)
 WIDE = len(CHUNKS) - 1
@@ -41,33 +38,34 @@ def tile_picked_interl_none_p_kernel(
         held = ctx.enter_context(tc.tile_pool(name="held", bufs=1))
         psum = ctx.enter_context(tc.psum_pool(name="psum", bufs=PSUM_BANKS))
 
+        def sbuf(shape, dtype, name, on=None):
+            return held.tile(shape, dtype, name=name, tag=on or name, align_bytes=64)
+
         def load_list(source, name):
             tile = held.tile([P, S // 16], U16, name=name)
             nc.sync.dma_start(tile[:], source)
             return tile
 
         def load_weight(source, name):
-            tile = held.tile([P, PACK, H], F32, name=name, align_bytes=64)
+            tile = sbuf([P, PACK, H], F32, name)
             nc.sync.dma_start(tile[:], source.rearrange("(p j) c -> p j c", j=PACK))
             return tile
 
         def gather(table, offsets, dtype, name):
-            picked = held.tile([P, S], dtype, name=name, align_bytes=64)
+            picked = sbuf([P, S], dtype, name)
             vector_copy(picked[:], table[:].indirect(offsets[:]))
             return picked
 
-        def mx_tiles(width, name):
-            words = held.tile([P, width], U32, name=name + "_words", align_bytes=64)
-            scales = held.tile([P, width], U8, name=name + "_scales", align_bytes=64)
-            return words, scales
+        def mx_tiles(width, name, on=None):
+            return sbuf([P, width], U32, name + "_words", on), sbuf([P, width], U8, name + "_scales")
 
         def quantise_into(target, columns, values):
             nc.vector.quantize_mx(
                 out=target[0][:, columns].bitcast(FP8X4), scales=target[1][:, columns], in_=values
             )
 
-        def quantise(values, name):
-            target = mx_tiles(values.shape[1] // PACK, name)
+        def quantise(values, name, on=None):
+            target = mx_tiles(values.shape[1] // PACK, name, on)
             quantise_into(target, slice(None), values)
             return target
 
@@ -82,8 +80,8 @@ def tile_picked_interl_none_p_kernel(
                 stop=True,
             )
 
-        def project(weights, columns, moving, name, tag=None, parts=1):
-            values = held.tile([P, S], F32, name=name, tag=tag or name, align_bytes=64)
+        def project(weights, columns, moving, name, on=None, parts=1):
+            values = sbuf([P, S], F32, name, on)
             for part in range(parts):
                 tokens = block(part, S // parts)
                 bank = psum.tile([P, S // parts], F32, name="bank")
@@ -93,8 +91,10 @@ def tile_picked_interl_none_p_kernel(
 
         def round_plane(target, raw, t):
             scalar_copy(
-                target.rearrange("p (b r j) -> p b r j", r=BLOCK_ROWS, j=PACK),
-                raw[:].rearrange("p j (b t r) -> p t b r j", t=PACK, r=BLOCK_ROWS)[:, t],
+                target.rearrange("p (b h i j) -> p b h j i", h=BLOCK_ROWS // LINE, i=LINE, j=PACK),
+                raw[:].rearrange("p j (b t h i) -> p t b h j i", t=PACK, h=BLOCK_ROWS // LINE, i=LINE)[
+                    :, t
+                ],
             )
 
         scale_rows = held.tile([P, T], U8, name="scale_rows")
@@ -113,7 +113,7 @@ def tile_picked_interl_none_p_kernel(
         text_places = load_list(la, "text_places")
         w2_raw = load_weight(w2, "w2_raw")
         image_places = load_list(lb, "image_places")
-        w3_raw = held.tile([P, PACK, N], F32, name="w3_raw", align_bytes=64)
+        w3_raw = sbuf([P, PACK, N], F32, "w3_raw")
         for t in range(PACK):
             nc.sync.dma_start(
                 w3_raw[:, t, :],
@@ -128,12 +128,12 @@ def tile_picked_interl_none_p_kernel(
         image_scales = gather(table_scales, image_list, U8, "image_scales")
 
         w1_mx = {}
-        for t in PLANES:
-            w1_bf = held.tile([P, P * PACK], BF16, name="w1_bf%d" % t, align_bytes=64)
+        for t in (1, 3, 2, 0):
+            w1_bf = sbuf([P, P * PACK], BF16, "w1_bf%d" % t)
             round_plane(w1_bf[:], w1_raw, t)
             w1_mx[t] = quantise(w1_bf[:], "w1_%d" % t)
 
-        text_words = held.tile([P, S], U32, name="text_words", align_bytes=64)
+        text_words = sbuf([P, S], U32, "text_words")
         for half in range(2):
             vector_copy(
                 text_words[:, block(half, S // 2)],
@@ -142,56 +142,61 @@ def tile_picked_interl_none_p_kernel(
         text = (text_words, text_scales)
         image = (gather(table_words, image_list, U32, "image_words"), image_scales)
 
-        y = {}
-        z = {
-            t: held.tile([P, U if t % 2 else 2 * U], F32, name="z%d" % t, align_bytes=64)
-            for t in PLANES
-        }
-
-        def project_text(t, tag=None, parts=1):
-            y[t] = project(w1_mx[t], block(0), text, "y%d" % t, tag, parts)
+        z = {t: sbuf([P, U if t % 2 else 2 * U], F32, "z%d" % t) for t in range(PACK)}
+        y, e = {}, {}
 
         def place_text(t):
             vector_copy(z[t][:].indirect(text_places[:]), y[t][:])
 
-        project_text(FIRST, parts=2)
-        project_text(SECOND)
-        for t in (FIRST, SECOND):
-            place_text(t)
+        def place_image(t):
+            vector_copy(z[t][:].indirect(image_places[:]), e[t][:])
 
-        w2_bf = held.tile([P, PACK * H], BF16, name="w2_bf", align_bytes=64)
-        for t in PLANES:
+        y[1] = project(w1_mx[1], block(0), text, "y1", parts=2)
+        y[3] = project(w1_mx[3], block(0), text, "y3")
+        place_text(1)
+        place_text(3)
+
+        w2_bf = sbuf([P, PACK * H], BF16, "w2_bf")
+        for t in (1, 3, 2, 0):
             round_plane(w2_bf[:, block(t, P * PACK)], w2_raw, t)
         w2_mx = quantise(w2_bf[:], "w2")
 
-        project_text(THIRD, tag="w2_raw")
-        place_text(THIRD)
+        y[2] = project(w1_mx[2], block(0), text, "y2", on="w2_raw")
+        place_text(2)
+        for t in (1, 3, 2):
+            e[t] = project(w2_mx, block(t), image, "e%d" % t)
+        y[0] = project(w1_mx[0], block(0), text, "y0")
 
-        starts = [sum(CHUNKS[:i]) for i in range(len(CHUNKS))]
-        z_bf = [
-            held.tile([P, width, PACK], BF16, name="z_bf%d" % i, align_bytes=64)
-            for i, width in enumerate(CHUNKS)
-        ]
+        w3_bf = [sbuf([P, N // 2, PACK], BF16, "w3_bf%d" % half) for half in range(2)]
 
-        e = {t: project(w2_mx, block(t), image, "e%d" % t) for t in (FIRST, SECOND, THIRD)}
-
-        w3_bf = [
-            held.tile([P, N // 2, PACK], BF16, name="w3_bf%d" % half, align_bytes=64)
-            for half in range(2)
-        ]
-        early, late = slice(LATE, None), slice(0, LATE)
-
-        def round_w3(half, columns):
+        def round_w3(half, first, end):
             scalar_copy(
-                w3_bf[half][:, columns, :],
-                w3_raw[:, :, block(half, N // 2)].rearrange("p t c -> p c t")[:, columns, :],
+                w3_bf[half][:, first:end, :].rearrange("p (c i) t -> p c t i", i=LINE),
+                w3_raw[:, :, block(half, N // 2)][:, :, first:end].rearrange(
+                    "p t (c i) -> p c t i", i=LINE
+                ),
             )
 
-        def quantise_w3(half):
-            return quantise(w3_bf[half][:].rearrange("p c t -> p (c t)"), "w3_%d" % half)
+        def quantise_w3(half, on=None):
+            return quantise(w3_bf[half][:].rearrange("p c t -> p (c t)"), "w3_%d" % half, on)
 
-        def place_image(t):
-            vector_copy(z[t][:].indirect(image_places[:]), e[t][:])
+        round_w3(0, LATE, N // 2)
+        round_w3(1, 0, N // 2)
+
+        place_image(1)
+        place_image(3)
+        scalar_copy(z[0][:, U : 2 * U - LATE], z[1][:, : U - LATE])
+        place_text(0)
+        scalar_copy(z[2][:, U:], z[3][:])
+        place_image(2)
+        e[0] = project(w2_mx, block(0), image, "e0", on="z3")
+        place_image(0)
+        round_w3(0, 0, LATE)
+        w3_mx = [quantise_w3(0)]
+
+        starts = [sum(CHUNKS[:i]) for i in range(len(CHUNKS))]
+        z_bf = [sbuf([P, width, PACK], BF16, "z_bf%d" % i) for i, width in enumerate(CHUNKS)]
+        z_mx = [mx_tiles(HALF, "z_mx%d" % half) for half in range(2)]
 
         def round_pair(copy, t, i, first=0, end=None):
             end = CHUNKS[i] if end is None else end
@@ -199,33 +204,6 @@ def tile_picked_interl_none_p_kernel(
                 z_bf[i][:, first:end, t : t + 2],
                 z[t][:].rearrange("p (s c) -> p c s", s=2)[:, starts[i] + first : starts[i] + end, :],
             )
-
-        project_text(LAST)
-        for half in range(2):
-            round_w3(half, early)
-
-        place_image(FIRST)
-        scalar_copy(z[THIRD][:, U:], z[FIRST][:])
-        place_image(SECOND)
-        scalar_copy(z[LAST][:, U:], z[SECOND][:])
-        last_bank = psum.tile([P, S], F32, name="bank")
-        multiply(last_bank[:], w2_mx, block(LAST), image)
-        e[LAST] = held.tile([P, S], F32, name="e_last", tag="z%d" % SECOND, align_bytes=64)
-        scalar_copy(e[LAST][:, early], last_bank[:, early])
-        round_w3(0, late)
-        place_image(THIRD)
-        for i in (WIDE, 0, 1):
-            round_pair(scalar_copy, THIRD, i)
-        scalar_copy(e[LAST][:, late], last_bank[:, late])
-        round_w3(1, late)
-        for i in (2, 3):
-            round_pair(scalar_copy, THIRD, i)
-        place_text(LAST)
-        w3_mx = [quantise_w3(0)]
-        place_image(LAST)
-        w3_mx.append(quantise_w3(1))
-
-        z_mx = [mx_tiles(HALF, "z_mx%d" % half) for half in range(2)]
 
         def quantise_chunk(i):
             first = starts[i] % HALF
@@ -247,13 +225,18 @@ def tile_picked_interl_none_p_kernel(
                 nc.sync.dma_start(out[block(m), block(half, HALF)][:, columns], result[:, columns])
 
         for i in range(WIDE):
-            round_pair((vector_copy, scalar_copy)[i % 2], LAST, i)
+            round_pair(scalar_copy, 2, i)
+        round_pair(scalar_copy, 2, WIDE, first=SCALAR_SHARE)
+        for i in range(WIDE):
+            round_pair((vector_copy, scalar_copy)[i // 2], 0, i)
+        scalar_copy(z[0][:, 2 * U - LATE :], z[1][:, U - LATE :])
         for i in range(WIDE):
             quantise_chunk(i)
-        round_pair(scalar_copy, LAST, WIDE, first=HALF - SCALAR_SHARE)
+        for t in (2, 0):
+            round_pair(scalar_copy, t, WIDE, end=SCALAR_SHARE)
+        w3_mx.append(quantise_w3(1, on="z_bf2"))
         produce(0, 0, [scalar_copy] * WIDE, stores=2)
-        for first, end in ((0, P), (P, 2 * P), (2 * P, HALF - SCALAR_SHARE)):
-            round_pair(vector_copy, LAST, WIDE, first, end)
+        round_pair(vector_copy, 0, WIDE, first=SCALAR_SHARE)
         produce(0, 1, [vector_copy, scalar_copy])
         quantise_chunk(WIDE)
         produce(0, 2, [scalar_copy, scalar_copy])

@@ -20,8 +20,8 @@ LINE = 4
 PSUM_BANKS = 8
 LATE = 16
 HALF = U // 2
-CHUNKS = (P, P, P, P, HALF)
-WIDE = len(CHUNKS) - 1
+CHUNKS = (P, P, P, P, 2 * P, 2 * P)
+WIDE = 4
 SCALAR_SHARE = 64
 
 
@@ -185,7 +185,11 @@ def tile_picked_interl_none_p_kernel(
 
         place_image(1)
         place_image(3)
-        scalar_copy(z[0][:, U : 2 * U - LATE], z[1][:, : U - LATE])
+        border = U - 2 * P
+        early = (slice(0, border - LATE), slice(border + LATE, U))
+        late = slice(border - LATE, border + LATE)
+        for columns in early:
+            scalar_copy(z[0][:, U:][:, columns], z[1][:, columns])
         place_text(0)
         scalar_copy(z[2][:, U:], z[3][:])
         place_image(2)
@@ -227,9 +231,10 @@ def tile_picked_interl_none_p_kernel(
         for i in range(WIDE):
             round_pair(scalar_copy, 2, i)
         round_pair(scalar_copy, 2, WIDE, first=SCALAR_SHARE)
+        round_pair(scalar_copy, 2, WIDE + 1)
         for i in range(WIDE):
             round_pair((vector_copy, scalar_copy)[i // 2], 0, i)
-        scalar_copy(z[0][:, 2 * U - LATE :], z[1][:, U - LATE :])
+        scalar_copy(z[0][:, U:][:, late], z[1][:, late])
         for i in range(WIDE):
             quantise_chunk(i)
         for t in (2, 0):
@@ -237,9 +242,11 @@ def tile_picked_interl_none_p_kernel(
         w3_mx.append(quantise_w3(1, on="z_bf2"))
         produce(0, 0, [scalar_copy] * WIDE, stores=2)
         round_pair(vector_copy, 0, WIDE, first=SCALAR_SHARE)
+        round_pair(vector_copy, 0, WIDE + 1)
         produce(0, 1, [vector_copy, scalar_copy])
         quantise_chunk(WIDE)
+        quantise_chunk(WIDE + 1)
         produce(0, 2, [scalar_copy, scalar_copy])
-        produce(0, 3, [vector_copy, scalar_copy])
+        produce(0, 3, [vector_copy, vector_copy])
         for m in range(N // P):
-            produce(1, m, [vector_copy, scalar_copy])
+            produce(1, m, [scalar_copy, vector_copy])

@@ -193,7 +193,7 @@ def tile_picked_interl_none_p_kernel(
         place_text(0)
         scalar_copy(z[2][:, U:], z[3][:])
         place_image(2)
-        e[0] = project(w2_mx, block(0), image, "e0", on="z3")
+        e[0] = project(w2_mx, block(0), image, "e0", on="e3")
         place_image(0)
         round_w3(0, 0, LATE)
         w3_mx = [quantise_w3(0)]

@@ -23,6 +23,8 @@ HALF = U // 2
 CHUNKS = (P, P, P, P, 2 * P, 2 * P)
 WIDE = 4
 SCALAR_SHARE = 64
+VECTOR_SHARE = 48
+DEFERRED = 96
 
 
 def block(index, width=P):
@@ -230,15 +232,18 @@ def tile_picked_interl_none_p_kernel(
 
         for i in range(WIDE):
             round_pair(scalar_copy, 2, i)
-        round_pair(scalar_copy, 2, WIDE, first=SCALAR_SHARE)
+        round_pair(scalar_copy, 2, WIDE, first=DEFERRED)
         round_pair(scalar_copy, 2, WIDE + 1)
-        for i in range(WIDE):
-            round_pair((vector_copy, scalar_copy)[i // 2], 0, i)
+        round_pair(vector_copy, 0, 0)
+        round_pair(vector_copy, 0, 1)
+        round_pair(vector_copy, 0, 2, end=VECTOR_SHARE)
+        round_pair(scalar_copy, 0, 2, first=VECTOR_SHARE)
+        round_pair(scalar_copy, 0, 3)
         scalar_copy(z[0][:, U:][:, late], z[1][:, late])
         for i in range(WIDE):
             quantise_chunk(i)
-        for t in (2, 0):
-            round_pair(scalar_copy, t, WIDE, end=SCALAR_SHARE)
+        round_pair(scalar_copy, 2, WIDE, end=DEFERRED)
+        round_pair(scalar_copy, 0, WIDE, end=SCALAR_SHARE)
         w3_mx.append(quantise_w3(1, on="z_bf2"))
         produce(0, 0, [scalar_copy] * WIDE, stores=2)
         round_pair(vector_copy, 0, WIDE, first=SCALAR_SHARE)

@@ -219,13 +219,15 @@ def tile_picked_interl_none_p_kernel(
                 z_bf[i][:].rearrange("p c t -> p (c t)"),
             )
 
-        def produce(half, m, copies, stores=1):
+        def produce(half, m, pieces, stores=1):
             result = held.tile([P, HALF], F32, name="result%d_%d" % (half, m))
-            width = HALF // len(copies)
-            for part, copy in enumerate(copies):
+            first = 0
+            for width, copy in pieces:
+                columns = slice(first, first + width)
                 bank = psum.tile([P, width], F32, name="bank")
-                multiply(bank[:], w3_mx[m // 2], block(m % 2), z_mx[half], block(part, width))
-                copy(result[:, block(part, width)], bank[:])
+                multiply(bank[:], w3_mx[m // 2], block(m % 2), z_mx[half], columns)
+                copy(result[:, columns], bank[:])
+                first = first + width
             for part in range(stores):
                 columns = block(part, HALF // stores)
                 nc.sync.dma_start(out[block(m), block(half, HALF)][:, columns], result[:, columns])
@@ -245,13 +247,13 @@ def tile_picked_interl_none_p_kernel(
         round_pair(scalar_copy, 2, WIDE, end=DEFERRED)
         round_pair(scalar_copy, 0, WIDE, end=SCALAR_SHARE)
         w3_mx.append(quantise_w3(1, on="z_bf2"))
-        produce(0, 0, [scalar_copy] * WIDE, stores=2)
+        produce(0, 0, [(P, scalar_copy)] * WIDE, stores=2)
         round_pair(vector_copy, 0, WIDE, first=SCALAR_SHARE)
         round_pair(vector_copy, 0, WIDE + 1)
-        produce(0, 1, [vector_copy, scalar_copy])
+        produce(0, 1, [(2 * P, vector_copy), (P, scalar_copy), (P, scalar_copy)])
         quantise_chunk(WIDE)
         quantise_chunk(WIDE + 1)
-        produce(0, 2, [scalar_copy, scalar_copy])
-        produce(0, 3, [vector_copy, vector_copy])
+        produce(0, 2, [(2 * P, scalar_copy), (2 * P, scalar_copy)])
+        produce(0, 3, [(2 * P, vector_copy), (2 * P, vector_copy)])
         for m in range(N // P):
-            produce(1, m, [scalar_copy, vector_copy])
+            produce(1, m, [(2 * P, scalar_copy), (2 * P, vector_copy)])

@@ -12,23 +12,26 @@ U32 = mybir.dt.uint32
 U16 = mybir.dt.uint16
 U8 = mybir.dt.uint8
 FP8X4 = mybir.dt.float8_e4m3fn_x4
+COPY = mybir.ActivationFunctionType.Copy
 
 P = 128
 PACK = 4
-BLOCK_ROWS = 8
 LINE = 4
 PSUM_BANKS = 8
-LATE = 16
 HALF = U // 2
 CHUNKS = (P, P, P, P, 2 * P, 2 * P)
 WIDE = 4
 SCALAR_SHARE = 64
 VECTOR_SHARE = 48
-DEFERRED = 96
+FIRST = (slice(0, S // 2), slice(S // 2, S))
 
 
 def block(index, width=P):
     return slice(width * index, width * (index + 1))
+
+
+def entries(offsets, tokens):
+    return offsets[:, tokens.start // 16 : tokens.stop // 16]
 
 
 def tile_picked_interl_none_p_kernel(
@@ -36,6 +39,13 @@ def tile_picked_interl_none_p_kernel(
 ):
     nc = tc.nc
     vector_copy, scalar_copy = nc.vector.tensor_copy, nc.scalar.copy
+
+    def scalar_activation(target, source):
+        nc.scalar.activation(target, source, COPY)
+
+    def gpsimd_copy(target, source):
+        nc.gpsimd.tensor_scalar(target, source, 1.0, 0.0, mybir.AluOpType.mult, mybir.AluOpType.add)
+
     with ExitStack() as ctx:
         held = ctx.enter_context(tc.tile_pool(name="held", bufs=1))
         psum = ctx.enter_context(tc.psum_pool(name="psum", bufs=PSUM_BANKS))
@@ -82,21 +92,20 @@ def tile_picked_interl_none_p_kernel(
                 stop=True,
             )
 
-        def project(weights, columns, moving, name, on=None, parts=1):
-            values = sbuf([P, S], F32, name, on)
-            for part in range(parts):
-                tokens = block(part, S // parts)
-                bank = psum.tile([P, S // parts], F32, name="bank")
-                multiply(bank[:], weights, columns, moving, tokens)
-                scalar_copy(values[:, tokens], bank[:])
+        def project_into(values, copy, weights, columns, moving, tokens=slice(None)):
+            bank = psum.tile([P, values.shape[1]], F32, name="bank")
+            multiply(bank[:], weights, columns, moving, tokens)
+            copy(values, bank[:])
+
+        def project(copy, weights, columns, moving, name, on=None, tokens=slice(0, S)):
+            values = sbuf([P, tokens.stop - tokens.start], F32, name, on)
+            project_into(values[:], copy, weights, columns, moving, tokens)
             return values
 
-        def round_plane(target, raw, t):
-            scalar_copy(
-                target.rearrange("p (b h i j) -> p b h j i", h=BLOCK_ROWS // LINE, i=LINE, j=PACK),
-                raw[:].rearrange("p j (b t h i) -> p t b h j i", t=PACK, h=BLOCK_ROWS // LINE, i=LINE)[
-                    :, t
-                ],
+        def round_planes(copy, target, raw, first, end):
+            copy(
+                target[:].rearrange("p (t g i j) -> p g t j i", t=end - first, i=LINE, j=PACK),
+                raw[:].rearrange("p j (g t i) -> p g t j i", t=PACK, i=LINE)[:, :, first:end],
             )
 
         scale_rows = held.tile([P, T], U8, name="scale_rows")
@@ -119,7 +128,7 @@ def tile_picked_interl_none_p_kernel(
         for t in range(PACK):
             nc.sync.dma_start(
                 w3_raw[:, t, :],
-                w3.rearrange("(b t r) c -> t b r c", t=PACK, r=BLOCK_ROWS)[t],
+                w3.rearrange("(g t i) c -> t g i c", t=PACK, i=LINE)[t],
             )
 
         table_scales = held.tile([P, T], U8, name="table_scales")
@@ -130,78 +139,63 @@ def tile_picked_interl_none_p_kernel(
         image_scales = gather(table_scales, image_list, U8, "image_scales")
 
         w1_mx = {}
-        for t in (1, 3, 2, 0):
-            w1_bf = sbuf([P, P * PACK], BF16, "w1_bf%d" % t)
-            round_plane(w1_bf[:], w1_raw, t)
+        for t in (3, 1, 0, 2):
+            w1_bf = sbuf([P, H], BF16, "w1_bf%d" % t)
+            scalar_activation(
+                w1_bf[:].rearrange("p (g i j) -> p g j i", i=LINE, j=PACK),
+                w1_raw[:].rearrange("p j (g t i) -> p t g j i", t=PACK, i=LINE)[:, t],
+            )
             w1_mx[t] = quantise(w1_bf[:], "w1_%d" % t)
 
         text_words = sbuf([P, S], U32, "text_words")
-        for half in range(2):
-            vector_copy(
-                text_words[:, block(half, S // 2)],
-                table_words[:].indirect(text_list[:, block(half, S // 32)]),
-            )
+        for tokens in FIRST:
+            vector_copy(text_words[:, tokens], table_words[:].indirect(entries(text_list, tokens)))
         text = (text_words, text_scales)
         image = (gather(table_words, image_list, U32, "image_words"), image_scales)
 
-        z = {t: sbuf([P, U if t % 2 else 2 * U], F32, "z%d" % t) for t in range(PACK)}
-        y, e = {}, {}
+        z = {t: sbuf([P, 2 * U], F32, "z%d" % t) for t in (0, 2)}
+        z[3] = sbuf([P, U], F32, "z3")
 
-        def place_text(t):
-            vector_copy(z[t][:].indirect(text_places[:]), y[t][:])
+        for tokens in FIRST:
+            values = project(scalar_copy, w1_mx[3], block(0), text, "y3_%d" % tokens.start, tokens=tokens)
+            scalar_activation(z[3][:].indirect(entries(text_places, tokens)), values[:])
+        y1 = project(vector_copy, w1_mx[1], block(0), text, "y1")
 
-        def place_image(t):
-            vector_copy(z[t][:].indirect(image_places[:]), e[t][:])
+        w2_last = sbuf([P, H], BF16, "w2_last")
+        w2_rest = sbuf([P, 3 * H], BF16, "w2_rest")
+        round_planes(vector_copy, w2_last, w2_raw, 3, 4)
+        round_planes(vector_copy, w2_rest, w2_raw, 0, 3)
+        w2_mx3 = quantise(w2_last[:], "w2_3")
+        w2_mx = quantise(w2_rest[:], "w2")
 
-        y[1] = project(w1_mx[1], block(0), text, "y1", parts=2)
-        y[3] = project(w1_mx[3], block(0), text, "y3")
-        place_text(1)
-        place_text(3)
+        z[1] = sbuf([P, U], F32, "z1", on="w2_raw")
+        vector_copy(z[1][:].indirect(text_places[:]), y1[:])
+        e3 = project(scalar_copy, w2_mx3, block(0), image, "e3")
+        scalar_activation(z[3][:].indirect(image_places[:]), e3[:])
+        nc.sync.dma_start(z[2][:, U:], z[3][:])
+        e1 = project(vector_copy, w2_mx, block(1), image, "e1")
+        y0 = project(vector_copy, w1_mx[0], block(0), text, "y0", on="y1")
+        scalar_activation(z[0][:].indirect(text_places[:]), y0[:])
+        y2 = project(vector_copy, w1_mx[2], block(0), text, "y2")
+        vector_copy(z[1][:].indirect(image_places[:]), e1[:])
+        e0 = project(vector_copy, w2_mx, block(0), image, "e0", on="e1")
+        e2 = project(vector_copy, w2_mx, block(2), image, "e2", on="e3")
+        vector_copy(z[0][:, U:], z[1][:])
+        vector_copy(z[0][:].indirect(image_places[:]), e0[:])
 
-        w2_bf = sbuf([P, PACK * H], BF16, "w2_bf")
-        for t in (1, 3, 2, 0):
-            round_plane(w2_bf[:, block(t, P * PACK)], w2_raw, t)
-        w2_mx = quantise(w2_bf[:], "w2")
-
-        y[2] = project(w1_mx[2], block(0), text, "y2", on="w2_raw")
-        place_text(2)
-        for t in (1, 3, 2):
-            e[t] = project(w2_mx, block(t), image, "e%d" % t)
-        y[0] = project(w1_mx[0], block(0), text, "y0")
-
-        w3_bf = [sbuf([P, N // 2, PACK], BF16, "w3_bf%d" % half) for half in range(2)]
-
-        def round_w3(half, first, end):
-            scalar_copy(
-                w3_bf[half][:, first:end, :].rearrange("p (c i) t -> p c t i", i=LINE),
-                w3_raw[:, :, block(half, N // 2)][:, :, first:end].rearrange(
-                    "p t (c i) -> p c t i", i=LINE
-                ),
+        w3_bf = sbuf([P, N, PACK], BF16, "w3_bf", on="w2_rest")
+        for m in range(N // P):
+            gpsimd_copy(
+                w3_bf[:, block(m), :].rearrange("p (c i) t -> p c t i", i=LINE),
+                w3_raw[:, :, block(m)].rearrange("p t (c i) -> p c t i", i=LINE),
             )
+        w3_mx = quantise(w3_bf[:].rearrange("p c t -> p (c t)"), "w3", on="w2_raw")
 
-        def quantise_w3(half, on=None):
-            return quantise(w3_bf[half][:].rearrange("p c t -> p (c t)"), "w3_%d" % half, on)
-
-        round_w3(0, LATE, N // 2)
-        round_w3(1, 0, N // 2)
-
-        place_image(1)
-        place_image(3)
-        border = U - 2 * P
-        early = (slice(0, border - LATE), slice(border + LATE, U))
-        late = slice(border - LATE, border + LATE)
-        for columns in early:
-            scalar_copy(z[0][:, U:][:, columns], z[1][:, columns])
-        place_text(0)
-        scalar_copy(z[2][:, U:], z[3][:])
-        place_image(2)
-        e[0] = project(w2_mx, block(0), image, "e0", on="e3")
-        place_image(0)
-        round_w3(0, 0, LATE)
-        w3_mx = [quantise_w3(0)]
+        scalar_activation(z[2][:].indirect(text_places[:]), y2[:])
+        scalar_activation(z[2][:].indirect(image_places[:]), e2[:])
 
         starts = [sum(CHUNKS[:i]) for i in range(len(CHUNKS))]
-        z_bf = [sbuf([P, width, PACK], BF16, "z_bf%d" % i) for i, width in enumerate(CHUNKS)]
+        z_bf = {}
         z_mx = [mx_tiles(HALF, "z_mx%d" % half) for half in range(2)]
 
         def round_pair(copy, t, i, first=0, end=None):
@@ -225,7 +219,7 @@ def tile_picked_interl_none_p_kernel(
             for width, copy in pieces:
                 columns = slice(first, first + width)
                 bank = psum.tile([P, width], F32, name="bank")
-                multiply(bank[:], w3_mx[m // 2], block(m % 2), z_mx[half], columns)
+                multiply(bank[:], w3_mx, block(m), z_mx[half], columns)
                 copy(result[:, columns], bank[:])
                 first = first + width
             for part in range(stores):
@@ -233,27 +227,27 @@ def tile_picked_interl_none_p_kernel(
                 nc.sync.dma_start(out[block(m), block(half, HALF)][:, columns], result[:, columns])
 
         for i in range(WIDE):
-            round_pair(scalar_copy, 2, i)
-        round_pair(scalar_copy, 2, WIDE, first=DEFERRED)
-        round_pair(scalar_copy, 2, WIDE + 1)
-        round_pair(vector_copy, 0, 0)
-        round_pair(vector_copy, 0, 1)
-        round_pair(vector_copy, 0, 2, end=VECTOR_SHARE)
-        round_pair(scalar_copy, 0, 2, first=VECTOR_SHARE)
-        round_pair(scalar_copy, 0, 3)
-        scalar_copy(z[0][:, U:][:, late], z[1][:, late])
+            z_bf[i] = sbuf([P, CHUNKS[i], PACK], BF16, "z_bf%d" % i)
+            round_pair(vector_copy, 0, i)
+        round_pair(vector_copy, 2, 0)
+        round_pair(vector_copy, 2, 1)
+        round_pair(vector_copy, 2, 2, end=VECTOR_SHARE)
+        round_pair(scalar_copy, 2, 2, first=VECTOR_SHARE)
+        round_pair(scalar_copy, 2, 3)
         for i in range(WIDE):
             quantise_chunk(i)
-        round_pair(scalar_copy, 2, WIDE, end=DEFERRED)
-        round_pair(scalar_copy, 0, WIDE, end=SCALAR_SHARE)
-        w3_mx.append(quantise_w3(1, on="z_bf2"))
+        for i in (WIDE, WIDE + 1):
+            z_bf[i] = sbuf([P, CHUNKS[i], PACK], BF16, "z_bf%d" % i, on="z_bf%d" % (i - 2))
+        round_pair(scalar_copy, 2, WIDE, end=SCALAR_SHARE)
         produce(0, 0, [(P, scalar_copy)] * WIDE, stores=2)
-        round_pair(vector_copy, 0, WIDE, first=SCALAR_SHARE)
+        round_pair(vector_copy, 0, WIDE)
+        round_pair(vector_copy, 2, WIDE, first=SCALAR_SHARE)
         round_pair(vector_copy, 0, WIDE + 1)
-        produce(0, 1, [(2 * P, vector_copy), (P, scalar_copy), (P, scalar_copy)])
+        produce(0, 1, [(2 * P, scalar_copy), (2 * P, scalar_copy)])
         quantise_chunk(WIDE)
-        quantise_chunk(WIDE + 1)
+        round_pair(vector_copy, 2, WIDE + 1)
         produce(0, 2, [(2 * P, scalar_copy), (2 * P, scalar_copy)])
-        produce(0, 3, [(2 * P, vector_copy), (2 * P, vector_copy)])
+        quantise_chunk(WIDE + 1)
+        produce(0, 3, [(2 * P, scalar_copy), (2 * P, vector_copy)])
         for m in range(N // P):
             produce(1, m, [(2 * P, scalar_copy), (2 * P, vector_copy)])

@@ -21,8 +21,7 @@ PSUM_BANKS = 8
 HALF = U // 2
 CHUNKS = (P, P, P, P, 2 * P, 2 * P)
 WIDE = 4
-SCALAR_SHARE = 64
-VECTOR_SHARE = 48
+SCALAR_SHARE = P
 FIRST = (slice(0, S // 2), slice(S // 2, S))
 
 
@@ -139,7 +138,7 @@ def tile_picked_interl_none_p_kernel(
         image_scales = gather(table_scales, image_list, U8, "image_scales")
 
         w1_mx = {}
-        for t in (3, 1, 0, 2):
+        for t in (3, 2, 1, 0):
             w1_bf = sbuf([P, H], BF16, "w1_bf%d" % t)
             scalar_activation(
                 w1_bf[:].rearrange("p (g i j) -> p g j i", i=LINE, j=PACK),
@@ -153,46 +152,50 @@ def tile_picked_interl_none_p_kernel(
         text = (text_words, text_scales)
         image = (gather(table_words, image_list, U32, "image_words"), image_scales)
 
-        z = {t: sbuf([P, 2 * U], F32, "z%d" % t) for t in (0, 2)}
-        z[3] = sbuf([P, U], F32, "z3")
+        z = {t: sbuf([P, U if t % 2 else 2 * U], F32, "z%d" % t) for t in range(PACK)}
+        y = {t: sbuf([P, S], F32, "y%d" % t) for t in (2, 3)}
 
-        for tokens in FIRST:
-            values = project(scalar_copy, w1_mx[3], block(0), text, "y3_%d" % tokens.start, tokens=tokens)
-            scalar_activation(z[3][:].indirect(entries(text_places, tokens)), values[:])
-        y1 = project(vector_copy, w1_mx[1], block(0), text, "y1")
+        def stage(t, tokens):
+            project_into(y[t][:, tokens], scalar_copy, w1_mx[t], block(0), text, tokens)
 
-        w2_last = sbuf([P, H], BF16, "w2_last")
-        w2_rest = sbuf([P, 3 * H], BF16, "w2_rest")
-        round_planes(vector_copy, w2_last, w2_raw, 3, 4)
-        round_planes(vector_copy, w2_rest, w2_raw, 0, 3)
-        w2_mx3 = quantise(w2_last[:], "w2_3")
-        w2_mx = quantise(w2_rest[:], "w2")
+        def place(t, tokens):
+            scalar_activation(z[t][:].indirect(entries(text_places, tokens)), y[t][:, tokens])
 
-        z[1] = sbuf([P, U], F32, "z1", on="w2_raw")
-        vector_copy(z[1][:].indirect(text_places[:]), y1[:])
-        e3 = project(scalar_copy, w2_mx3, block(0), image, "e3")
+        stage(3, FIRST[0])
+        stage(2, FIRST[0])
+        place(3, FIRST[0])
+        stage(3, FIRST[1])
+        place(2, FIRST[0])
+        place(3, FIRST[1])
+
+        w2_bf = sbuf([P, PACK * H], BF16, "w2_bf")
+        round_planes(vector_copy, w2_bf, w2_raw, 0, PACK)
+        w2_mx = quantise(w2_bf[:], "w2")
+        y_low = sbuf([P, 2 * S], F32, "y_low", on="w2_raw")
+        for t in (1, 0):
+            project_into(y_low[:, block(t, S)], vector_copy, w1_mx[t], block(0), text)
+        for t in (1, 0):
+            vector_copy(z[t][:].indirect(text_places[:]), y_low[:, block(t, S)])
+
+        e3 = project(scalar_copy, w2_mx, block(3), image, "e3")
+        stage(2, FIRST[1])
         scalar_activation(z[3][:].indirect(image_places[:]), e3[:])
+        place(2, FIRST[1])
         nc.sync.dma_start(z[2][:, U:], z[3][:])
-        e1 = project(vector_copy, w2_mx, block(1), image, "e1")
-        y0 = project(vector_copy, w1_mx[0], block(0), text, "y0", on="y1")
-        scalar_activation(z[0][:].indirect(text_places[:]), y0[:])
-        y2 = project(vector_copy, w1_mx[2], block(0), text, "y2")
-        vector_copy(z[1][:].indirect(image_places[:]), e1[:])
-        e0 = project(vector_copy, w2_mx, block(0), image, "e0", on="e1")
-        e2 = project(vector_copy, w2_mx, block(2), image, "e2", on="e3")
-        vector_copy(z[0][:, U:], z[1][:])
-        vector_copy(z[0][:].indirect(image_places[:]), e0[:])
+        e = {t: project(vector_copy, w2_mx, block(t), image, "e%d" % t) for t in (1, 0, 2)}
+        scalar_activation(z[1][:].indirect(image_places[:]), e[1][:])
+        vector_copy(z[0][:].indirect(image_places[:]), e[0][:])
+        for half in range(2):
+            vector_copy(z[0][:, U:][:, block(half, HALF)], z[1][:, block(half, HALF)])
 
-        w3_bf = sbuf([P, N, PACK], BF16, "w3_bf", on="w2_rest")
+        w3_bf = sbuf([P, N, PACK], BF16, "w3_bf", on="w2_bf")
         for m in range(N // P):
             gpsimd_copy(
                 w3_bf[:, block(m), :].rearrange("p (c i) t -> p c t i", i=LINE),
                 w3_raw[:, :, block(m)].rearrange("p t (c i) -> p c t i", i=LINE),
             )
-        w3_mx = quantise(w3_bf[:].rearrange("p c t -> p (c t)"), "w3", on="w2_raw")
-
-        scalar_activation(z[2][:].indirect(text_places[:]), y2[:])
-        scalar_activation(z[2][:].indirect(image_places[:]), e2[:])
+        w3_mx = quantise(w3_bf[:].rearrange("p c t -> p (c t)"), "w3")
+        scalar_activation(z[2][:].indirect(image_places[:]), e[2][:])
 
         starts = [sum(CHUNKS[:i]) for i in range(len(CHUNKS))]
         z_bf = {}
@@ -226,28 +229,36 @@ def tile_picked_interl_none_p_kernel(
                 columns = block(part, HALF // stores)
                 nc.sync.dma_start(out[block(m), block(half, HALF)][:, columns], result[:, columns])
 
+        def produce_quarter(quarter, copies):
+            columns = block(quarter, 2 * P)
+            result = held.tile([P, PACK, 2 * P], F32, name="quarter%d" % quarter)
+            for m, copy in enumerate(copies):
+                bank = psum.tile([P, 2 * P], F32, name="bank")
+                multiply(bank[:], w3_mx, block(m), z_mx[0], columns)
+                copy(result[:, m, :], bank[:])
+                if m % 2:
+                    pair = block(m // 2, 2)
+                    nc.sync.dma_start(
+                        out.rearrange("(m p) c -> p m c", p=P)[:, pair, columns], result[:, pair, :]
+                    )
+
         for i in range(WIDE):
             z_bf[i] = sbuf([P, CHUNKS[i], PACK], BF16, "z_bf%d" % i)
             round_pair(vector_copy, 0, i)
-        round_pair(vector_copy, 2, 0)
-        round_pair(vector_copy, 2, 1)
-        round_pair(vector_copy, 2, 2, end=VECTOR_SHARE)
-        round_pair(scalar_copy, 2, 2, first=VECTOR_SHARE)
-        round_pair(scalar_copy, 2, 3)
+        for i in range(WIDE):
+            round_pair((vector_copy, scalar_copy)[i % 2], 2, i)
         for i in range(WIDE):
             quantise_chunk(i)
         for i in (WIDE, WIDE + 1):
             z_bf[i] = sbuf([P, CHUNKS[i], PACK], BF16, "z_bf%d" % i, on="z_bf%d" % (i - 2))
         round_pair(scalar_copy, 2, WIDE, end=SCALAR_SHARE)
-        produce(0, 0, [(P, scalar_copy)] * WIDE, stores=2)
+        produce_quarter(0, (scalar_copy,) * 4)
         round_pair(vector_copy, 0, WIDE)
         round_pair(vector_copy, 2, WIDE, first=SCALAR_SHARE)
         round_pair(vector_copy, 0, WIDE + 1)
-        produce(0, 1, [(2 * P, scalar_copy), (2 * P, scalar_copy)])
         quantise_chunk(WIDE)
         round_pair(vector_copy, 2, WIDE + 1)
-        produce(0, 2, [(2 * P, scalar_copy), (2 * P, scalar_copy)])
+        produce_quarter(1, (scalar_copy,) * 4)
         quantise_chunk(WIDE + 1)
-        produce(0, 3, [(2 * P, scalar_copy), (2 * P, vector_copy)])
         for m in range(N // P):
             produce(1, m, [(2 * P, scalar_copy), (2 * P, vector_copy)])

@@ -19,9 +19,9 @@ PACK = 4
 LINE = 4
 PSUM_BANKS = 8
 HALF = U // 2
-CHUNKS = (P, P, P, P, 2 * P, 2 * P)
-WIDE = 4
-SCALAR_SHARE = P
+CHUNKS = (2 * P,) * 4
+VECTOR_SHARES = (128, 160)
+SCALAR_SHARE = 160
 FIRST = (slice(0, S // 2), slice(S // 2, S))
 
 
@@ -216,49 +216,35 @@ def tile_picked_interl_none_p_kernel(
                 z_bf[i][:].rearrange("p c t -> p (c t)"),
             )
 
-        def produce(half, m, pieces, stores=1):
+        def produce(half, m, copies):
             result = held.tile([P, HALF], F32, name="result%d_%d" % (half, m))
-            first = 0
-            for width, copy in pieces:
-                columns = slice(first, first + width)
-                bank = psum.tile([P, width], F32, name="bank")
+            for part, copy in enumerate(copies):
+                columns = block(part, 2 * P)
+                bank = psum.tile([P, 2 * P], F32, name="bank")
                 multiply(bank[:], w3_mx, block(m), z_mx[half], columns)
                 copy(result[:, columns], bank[:])
-                first = first + width
-            for part in range(stores):
-                columns = block(part, HALF // stores)
-                nc.sync.dma_start(out[block(m), block(half, HALF)][:, columns], result[:, columns])
+            nc.sync.dma_start(out[block(m), block(half, HALF)], result[:])
 
-        def produce_quarter(quarter, copies):
-            columns = block(quarter, 2 * P)
-            result = held.tile([P, PACK, 2 * P], F32, name="quarter%d" % quarter)
-            for m, copy in enumerate(copies):
-                bank = psum.tile([P, 2 * P], F32, name="bank")
-                multiply(bank[:], w3_mx, block(m), z_mx[0], columns)
-                copy(result[:, m, :], bank[:])
-                if m % 2:
-                    pair = block(m // 2, 2)
-                    nc.sync.dma_start(
-                        out.rearrange("(m p) c -> p m c", p=P)[:, pair, columns], result[:, pair, :]
-                    )
-
-        for i in range(WIDE):
+        for i in range(2):
             z_bf[i] = sbuf([P, CHUNKS[i], PACK], BF16, "z_bf%d" % i)
             round_pair(vector_copy, 0, i)
-        for i in range(WIDE):
-            round_pair((vector_copy, scalar_copy)[i % 2], 2, i)
-        for i in range(WIDE):
+        for i, share in enumerate(VECTOR_SHARES):
+            round_pair(vector_copy, 2, i, end=share)
+            round_pair(scalar_copy, 2, i, first=share)
+        for i in range(2):
             quantise_chunk(i)
-        for i in (WIDE, WIDE + 1):
+        for i in (2, 3):
             z_bf[i] = sbuf([P, CHUNKS[i], PACK], BF16, "z_bf%d" % i, on="z_bf%d" % (i - 2))
-        round_pair(scalar_copy, 2, WIDE, end=SCALAR_SHARE)
-        produce_quarter(0, (scalar_copy,) * 4)
-        round_pair(vector_copy, 0, WIDE)
-        round_pair(vector_copy, 2, WIDE, first=SCALAR_SHARE)
-        round_pair(vector_copy, 0, WIDE + 1)
-        quantise_chunk(WIDE)
-        round_pair(vector_copy, 2, WIDE + 1)
-        produce_quarter(1, (scalar_copy,) * 4)
-        quantise_chunk(WIDE + 1)
+        round_pair(scalar_copy, 2, 2, end=SCALAR_SHARE)
+        for m in range(2):
+            produce(0, m, (scalar_copy, scalar_copy))
+        round_pair(vector_copy, 0, 2)
+        round_pair(vector_copy, 0, 3)
+        round_pair(vector_copy, 2, 2, first=SCALAR_SHARE)
+        round_pair(vector_copy, 2, 3)
+        quantise_chunk(2)
+        quantise_chunk(3)
+        for m in range(2, N // P):
+            produce(0, m, (scalar_copy, scalar_copy))
         for m in range(N // P):
-            produce(1, m, [(2 * P, scalar_copy), (2 * P, vector_copy)])
+            produce(1, m, (scalar_copy, vector_copy))

from contextlib import ExitStack

import concourse.mybir as mybir

K, T, S, H, N, U = 512, 2048, 512, 512, 512, 1024
FLOPS = 2 * K * H * S * 2 + 2 * H * N * U

F32 = mybir.dt.float32
BF16 = mybir.dt.bfloat16
I32 = mybir.dt.int32
U32 = mybir.dt.uint32
U16 = mybir.dt.uint16
U8 = mybir.dt.uint8
FP8X4 = mybir.dt.float8_e4m3fn_x4
COPY = mybir.ActivationFunctionType.Copy

P = 128
PACK = 4
LINE = 4
PSUM_BANKS = 8
HALF = U // 2
CHUNKS = (2 * P,) * 4
VECTOR_SHARES = (128, 160)
SCALAR_SHARE = 160
FIRST = (slice(0, S // 2), slice(S // 2, S))


def block(index, width=P):
    return slice(width * index, width * (index + 1))


def entries(offsets, tokens):
    return offsets[:, tokens.start // 16 : tokens.stop // 16]


def tile_picked_interl_none_p_kernel(
    tc, x_words, x_scales, w1, w2, w3, offs, img, la, lb, out
):
    nc = tc.nc
    vector_copy, scalar_copy = nc.vector.tensor_copy, nc.scalar.copy

    def scalar_activation(target, source):
        nc.scalar.activation(target, source, COPY)

    def gpsimd_copy(target, source):
        nc.gpsimd.tensor_scalar(target, source, 1.0, 0.0, mybir.AluOpType.mult, mybir.AluOpType.add)

    with ExitStack() as ctx:
        held = ctx.enter_context(tc.tile_pool(name="held", bufs=1))
        psum = ctx.enter_context(tc.psum_pool(name="psum", bufs=PSUM_BANKS))

        def sbuf(shape, dtype, name, on=None):
            return held.tile(shape, dtype, name=name, tag=on or name, align_bytes=64)

        def load_list(source, name):
            tile = held.tile([P, S // 16], U16, name=name)
            nc.sync.dma_start(tile[:], source)
            return tile

        def load_weight(source, name):
            tile = sbuf([P, PACK, H], F32, name)
            nc.sync.dma_start(tile[:], source.rearrange("(p j) c -> p j c", j=PACK))
            return tile

        def gather(table, offsets, dtype, name):
            picked = sbuf([P, S], dtype, name)
            vector_copy(picked[:], table[:].indirect(offsets[:]))
            return picked

        def mx_tiles(width, name, on=None):
            return sbuf([P, width], U32, name + "_words", on), sbuf([P, width], U8, name + "_scales")

        def quantise_into(target, columns, values):
            nc.vector.quantize_mx(
                out=target[0][:, columns].bitcast(FP8X4), scales=target[1][:, columns], in_=values
            )

        def quantise(values, name, on=None):
            target = mx_tiles(values.shape[1] // PACK, name, on)
            quantise_into(target, slice(None), values)
            return target

        def multiply(target, stationary, columns, moving, tokens=slice(None)):
            nc.tensor.matmul_mx(
                out=target,
                lhsT=stationary[0][:, columns].bitcast(FP8X4),
                lhsT_scale=stationary[1][:, columns],
                rhs=moving[0][:, tokens].bitcast(FP8X4),
                rhs_scale=moving[1][:, tokens],
                start=True,
                stop=True,
            )

        def project_into(values, copy, weights, columns, moving, tokens=slice(None)):
            bank = psum.tile([P, values.shape[1]], F32, name="bank")
            multiply(bank[:], weights, columns, moving, tokens)
            copy(values, bank[:])

        def project(copy, weights, columns, moving, name, on=None, tokens=slice(0, S)):
            values = sbuf([P, tokens.stop - tokens.start], F32, name, on)
            project_into(values[:], copy, weights, columns, moving, tokens)
            return values

        def round_planes(copy, target, raw, first, end):
            copy(
                target[:].rearrange("p (t g i j) -> p g t j i", t=end - first, i=LINE, j=PACK),
                raw[:].rearrange("p j (g t i) -> p g t j i", t=PACK, i=LINE)[:, :, first:end],
            )

        scale_rows = held.tile([P, T], U8, name="scale_rows")
        quadrants = [slice(32 * q, 32 * q + 4) for q in range(4)]
        for q, rows in enumerate(quadrants):
            (nc.sync, nc.scalar)[q % 2].dma_start(
                scale_rows[rows, :].bitcast(I32), x_scales[0, 4 * q : 4 * q + 4, :].bitcast(I32)
            )
        text_list = load_list(offs, "text_list")
        w1_raw = load_weight(w1, "w1_raw")
        image_list = load_list(img, "image_list")
        table_words = held.tile([P, T], U32, name="table_words")
        nc.sync.dma_start(
            table_words[:].bitcast(I32), x_words[0].rearrange("p c r -> p (c r)").bitcast(I32)
        )
        text_places = load_list(la, "text_places")
        w2_raw = load_weight(w2, "w2_raw")
        image_places = load_list(lb, "image_places")
        w3_raw = sbuf([P, PACK, N], F32, "w3_raw")
        for t in range(PACK):
            nc.sync.dma_start(
                w3_raw[:, t, :],
                w3.rearrange("(g t i) c -> t g i c", t=PACK, i=LINE)[t],
            )

        table_scales = held.tile([P, T], U8, name="table_scales")
        nc.vector.memset(table_scales[:].bitcast(I32), 0)
        for rows in quadrants:
            vector_copy(table_scales[rows, :].bitcast(I32), scale_rows[rows, :].bitcast(I32))
        text_scales = gather(table_scales, text_list, U8, "text_scales")
        image_scales = gather(table_scales, image_list, U8, "image_scales")

        w1_mx = {}
        for t in (3, 2, 1, 0):
            w1_bf = sbuf([P, H], BF16, "w1_bf%d" % t)
            scalar_activation(
                w1_bf[:].rearrange("p (g i j) -> p g j i", i=LINE, j=PACK),
                w1_raw[:].rearrange("p j (g t i) -> p t g j i", t=PACK, i=LINE)[:, t],
            )
            w1_mx[t] = quantise(w1_bf[:], "w1_%d" % t)

        text_words = sbuf([P, S], U32, "text_words")
        for tokens in FIRST:
            vector_copy(text_words[:, tokens], table_words[:].indirect(entries(text_list, tokens)))
        text = (text_words, text_scales)
        image = (gather(table_words, image_list, U32, "image_words"), image_scales)

        z = {t: sbuf([P, U if t % 2 else 2 * U], F32, "z%d" % t) for t in range(PACK)}
        y = {t: sbuf([P, S], F32, "y%d" % t) for t in (2, 3)}

        def stage(t, tokens):
            project_into(y[t][:, tokens], scalar_copy, w1_mx[t], block(0), text, tokens)

        def place(t, tokens):
            scalar_activation(z[t][:].indirect(entries(text_places, tokens)), y[t][:, tokens])

        stage(3, FIRST[0])
        stage(2, FIRST[0])
        place(3, FIRST[0])
        stage(3, FIRST[1])
        place(2, FIRST[0])
        place(3, FIRST[1])

        w2_bf = sbuf([P, PACK * H], BF16, "w2_bf")
        round_planes(vector_copy, w2_bf, w2_raw, 0, PACK)
        w2_mx = quantise(w2_bf[:], "w2")
        y_low = sbuf([P, 2 * S], F32, "y_low", on="w2_raw")
        for t in (1, 0):
            project_into(y_low[:, block(t, S)], vector_copy, w1_mx[t], block(0), text)
        for t in (1, 0):
            vector_copy(z[t][:].indirect(text_places[:]), y_low[:, block(t, S)])

        e3 = project(scalar_copy, w2_mx, block(3), image, "e3")
        stage(2, FIRST[1])
        scalar_activation(z[3][:].indirect(image_places[:]), e3[:])
        place(2, FIRST[1])
        nc.sync.dma_start(z[2][:, U:], z[3][:])
        e = {t: project(vector_copy, w2_mx, block(t), image, "e%d" % t) for t in (1, 0, 2)}
        scalar_activation(z[1][:].indirect(image_places[:]), e[1][:])
        vector_copy(z[0][:].indirect(image_places[:]), e[0][:])
        for half in range(2):
            vector_copy(z[0][:, U:][:, block(half, HALF)], z[1][:, block(half, HALF)])

        w3_bf = sbuf([P, N, PACK], BF16, "w3_bf", on="w2_bf")
        for m in range(N // P):
            gpsimd_copy(
                w3_bf[:, block(m), :].rearrange("p (c i) t -> p c t i", i=LINE),
                w3_raw[:, :, block(m)].rearrange("p t (c i) -> p c t i", i=LINE),
            )
        w3_mx = quantise(w3_bf[:].rearrange("p c t -> p (c t)"), "w3")
        scalar_activation(z[2][:].indirect(image_places[:]), e[2][:])

        starts = [sum(CHUNKS[:i]) for i in range(len(CHUNKS))]
        z_bf = {}
        z_mx = [mx_tiles(HALF, "z_mx%d" % half) for half in range(2)]

        def round_pair(copy, t, i, first=0, end=None):
            end = CHUNKS[i] if end is None else end
            copy(
                z_bf[i][:, first:end, t : t + 2],
                z[t][:].rearrange("p (s c) -> p c s", s=2)[:, starts[i] + first : starts[i] + end, :],
            )

        def quantise_chunk(i):
            first = starts[i] % HALF
            quantise_into(
                z_mx[starts[i] // HALF],
                slice(first, first + CHUNKS[i]),
                z_bf[i][:].rearrange("p c t -> p (c t)"),
            )

        def produce(half, m, copies):
            result = held.tile([P, HALF], F32, name="result%d_%d" % (half, m))
            for part, copy in enumerate(copies):
                columns = block(part, 2 * P)
                bank = psum.tile([P, 2 * P], F32, name="bank")
                multiply(bank[:], w3_mx, block(m), z_mx[half], columns)
                copy(result[:, columns], bank[:])
            nc.sync.dma_start(out[block(m), block(half, HALF)], result[:])

        for i in range(2):
            z_bf[i] = sbuf([P, CHUNKS[i], PACK], BF16, "z_bf%d" % i)
            round_pair(vector_copy, 0, i)
        for i, share in enumerate(VECTOR_SHARES):
            round_pair(vector_copy, 2, i, end=share)
            round_pair(scalar_copy, 2, i, first=share)
        for i in range(2):
            quantise_chunk(i)
        for i in (2, 3):
            z_bf[i] = sbuf([P, CHUNKS[i], PACK], BF16, "z_bf%d" % i, on="z_bf%d" % (i - 2))
        round_pair(scalar_copy, 2, 2, end=SCALAR_SHARE)
        for m in range(2):
            produce(0, m, (scalar_copy, scalar_copy))
        round_pair(vector_copy, 0, 2)
        round_pair(vector_copy, 0, 3)
        round_pair(vector_copy, 2, 2, first=SCALAR_SHARE)
        round_pair(vector_copy, 2, 3)
        quantise_chunk(2)
        quantise_chunk(3)
        for m in range(2, N // P):
            produce(0, m, (scalar_copy, scalar_copy))
        for m in range(N // P):
            produce(1, m, (scalar_copy, vector_copy))
